import numpy as np
import ml_dtypes


def mxq(x, axis, fmt="e4m3"):
    dtype, down = {"e4m3": (ml_dtypes.float8_e4m3fn, 7), "e5m2": (ml_dtypes.float8_e5m2, 14)}[fmt]
    v = np.moveaxis(np.asarray(x, np.float32).astype(ml_dtypes.bfloat16).astype(np.float64), axis, -1)
    blocks = v.reshape(v.shape[:-1] + (-1, 32))
    amax = np.abs(blocks).max(-1, keepdims=True)
    byte = np.maximum(np.where(amax > 0, np.frexp(amax)[1] - 1 + 127, 0) - down, 1)
    scale = np.exp2(byte - 127.0)
    codes = (blocks / scale).astype(np.float32).astype(dtype).astype(np.float64)
    return np.moveaxis((codes * scale).reshape(v.shape), -1, axis)


WIDE = False


def mx_kscale(k):
    if not WIDE:
        return np.ones(k)
    levels = np.array([18, -18])
    if k % 512:
        return np.exp2(np.random.permutation(np.resize(levels, k // 32))).repeat(32)
    a = np.empty((k // 512, 16))
    for p in range(k // 512):
        a[p, :8] = np.random.permutation(np.resize(levels, 8))
        for g in range(8):
            far = levels[np.abs(levels - a[p, g]) >= 10]
            a[p, g + 8] = far[np.random.randint(len(far))]
    return np.exp2(a.ravel()).repeat(32)


def f64(x):
    return np.asarray(x).astype(np.float64)


def striped(idx):
    return np.tile(np.asarray(idx).reshape(-1, 16).T, (8, 1)).astype(np.uint16)


def unstriped(offs):
    return offs[:16].T.reshape(-1).astype(np.int64)


def sig(x):
    return 1.0 / (1.0 + np.exp(-x))


def setup_inputs():
    n = np.random.standard_normal
    uni = np.random.uniform
    idx = np.random.permutation(2048)[:512]
    f_d = mx_kscale(512)
    f_r = mx_kscale(512)
    return {
        "xT": (n((512, 512)) * f_d[:, None] * f_r[None, :]).astype(np.float32),
        "wT": (n((512, 2048)) / np.sqrt(512) / f_d[:, None]).astype(np.float32),
        "ts": np.tile(uni(0.75, 1.3, 2048), (128, 1)).astype(np.float32),
        "kb": np.tile(0.5 * n(2048), (128, 1)).astype(np.float32),
        "us": (uni(0.75, 1.3, (512, 1)) / f_r[:, None]).astype(np.float32),
        "y": (np.random.randint(0, 2, (512, 512))).astype(np.float32),
        "wt": (uni(0.75, 1.3, (512, 1)) / np.sqrt(512)).astype(np.float32),
        "offs": striped(idx),
    }


def reference(xT, wT, ts, kb, us, y, wt, offs):
    idx = unstriped(offs)
    wT_i = f64(wT)[:, idx]
    ts_i = f64(ts)[:1][:, idx]
    kb_i = f64(kb)[:1][:, idx]
    a = mxq(f64(xT), 0, "e4m3").T @ mxq(wT_i, 0, "e4m3")
    z = f64(us) * ts_i * a + kb_i
    g = f64(wt) * (sig(z) - f64(y))
    h = f64(us) * ts_i * g
    dw = mxq(f64(xT), 1, "e4m3") @ mxq(h, 0, "e5m2")
    out_0 = np.zeros((512, 2048))
    out_0[:, idx] = dw
    gt = g.T
    db = (gt).sum(-1, keepdims=True)
    out_1 = db.T
    return out_0, out_1

@@ -1,0 +1,232 @@
+from contextlib import ExitStack
+
+import concourse.mybir as mybir
+from concourse.masks import make_identity
+
+D, R, S, T = 512, 512, 512, 2048
+P = 128
+PACK = 4
+FLOPS = 2 * 2 * D * R * S
+BYTES = 4 * (D * R + D * T + 2 * T + 2 * R + R * S + D * T + S) + 2 * P * (S // 16)
+
+F32 = mybir.dt.float32
+BF16 = mybir.dt.bfloat16
+U32 = mybir.dt.uint32
+U16 = mybir.dt.uint16
+U8 = mybir.dt.uint8
+E4 = mybir.dt.float8_e4m3fn_x4
+E5 = mybir.dt.float8_e5m2_x4
+ACT = mybir.ActivationFunctionType
+ALU = mybir.AluOpType
+
+HALF = S // 2
+BLOCKS = S // P
+ROW = P - 1
+
+
+def tile_attend_gbias_wb_log_kernel(tc, xT, wT, ts, kb, us, y, wt, offs, out_0, out_1):
+    nc = tc.nc
+    with ExitStack() as ctx:
+        keep = ctx.enter_context(tc.tile_pool(name="keep", bufs=1))
+        psum = ctx.enter_context(tc.psum_pool(name="psum", bufs=4))
+
+        def sb(name, shape, dtype, tag=None):
+            return keep.tile(shape, dtype, name=name, tag=tag or name, align_bytes=64)
+
+        def bank(name, tag):
+            return psum.tile([P, PACK, P], F32, name=name, tag=tag)
+
+        def turn(out, in_, start=True, stop=True):
+            nc.tensor.matmul(out, in_, ident[:], start=start, stop=stop, is_transpose=True)
+
+        offsets = keep.tile([P, S // 16], U16, name="offsets")
+        x_raw = sb("x_raw", [P, PACK, R], F32)
+        y_raw = sb("y_raw", [P, PACK, S], F32)
+        w_raw = [sb("w_raw%d" % t, [P, T], F32) for t in range(PACK)]
+        ts_win = sb("ts_win", [P, T], F32)
+        kb_win = sb("kb_win", [P, T], F32)
+        us_col = sb("us_col", [P, PACK], F32)
+        wt_col = sb("wt_col", [P, PACK], F32)
+
+        nc.sync.dma_start(x_raw[:], xT.rearrange("(p t) r -> p t r", t=PACK))
+        nc.sync.dma_start(offsets[:], offs)
+        nc.scalar.dma_start(ts_win[ROW:P, :], ts[0:1, :])
+        nc.scalar.dma_start(kb_win[ROW:P, :], kb[0:1, :])
+        nc.sync.dma_start(us_col[:], us.rearrange("(p t) o -> p (t o)", t=PACK))
+        nc.sync.dma_start(wt_col[:], wt.rearrange("(p t) o -> p (t o)", t=PACK))
+        w_planes = wT.rearrange("(p t) c -> t p c", t=PACK)
+        for t in range(PACK):
+            nc.sync.dma_start(w_raw[t][:], w_planes[t])
+        nc.sync.dma_start(y_raw[:], y.rearrange("(p t) s -> p t s", t=PACK))
+
+        ident = sb("ident", [P, P], F32)
+        make_identity(nc, ident[:])
+        warm = sb("warm", [P, 1], F32)
+        nc.scalar.activation(warm[:], ident[:, 0:1], ACT.Sigmoid)
+
+        nc.vector.memset(ts_win[0:ROW, :], 0.0)
+        nc.vector.memset(kb_win[0:ROW, :], 0.0)
+        windows = [sb("window%d" % t, [P, T], F32) for t in range(PACK)]
+        for t in range(PACK):
+            for c0 in range(0, T, 1024):
+                nc.gpsimd.memset(windows[t][:, c0 : c0 + 1024], 0.0)
+
+        us_ps = bank("us_ps", "rot")
+        for t in range(PACK):
+            turn(us_ps[:, t, :], us_col[:, t : t + 1].to_broadcast([P, P]))
+        us_row = sb("us_row", [P, PACK, P], F32)
+        nc.scalar.copy(us_row[:], us_ps[:])
+        c_col = sb("c_col", [P, PACK], F32)
+        nc.vector.tensor_tensor(c_col[:], us_col[:], wt_col[:], ALU.mult)
+
+        cols = []
+        for name, win in (("ts", ts_win), ("kb", kb_win)):
+            picked = sb(name + "_picked", [P, S], F32)
+            nc.vector.tensor_copy(picked[:], win[:].indirect(offsets[:]))
+            col_ps = bank(name + "_ps", "rot")
+            for b in range(BLOCKS):
+                turn(col_ps[:, b, :], picked[:, b * P : (b + 1) * P])
+            col = sb(name + "_col", [P, BLOCKS], F32)
+            nc.scalar.copy(col[:], col_ps[:, :, ROW])
+            cols.append(col)
+        ts_col, kb_col = cols
+
+        x_d = sb("x_d", [P, R, PACK], BF16)
+        nc.scalar.copy(
+            x_d[:].rearrange("p (c i) t -> p c t i", i=4),
+            x_raw[:].rearrange("p t (c i) -> p c t i", i=4),
+        )
+        xd_codes = sb("xd_codes", [P, R], U32)
+        xd_scales = sb("xd_scales", [P, R], U8)
+        nc.vector.quantize_mx(xd_codes[:].bitcast(E4), xd_scales[:], x_d[:].rearrange("p r t -> p (r t)"))
+
+        x_r = sb("x_r", [P, D, PACK], BF16)
+        for t in range(PACK):
+            xt_ps = bank("xt_ps", "held")
+            for j in range(PACK):
+                turn(xt_ps[:, j, :], x_raw[:, t, j:R:PACK])
+            nc.scalar.copy(x_r[:, t * P : (t + 1) * P, :], xt_ps[:].rearrange("m j p -> m p j"))
+        xr_codes = sb("xr_codes", [P, D], U32)
+        xr_scales = sb("xr_scales", [P, D], U8)
+        nc.vector.quantize_mx(xr_codes[:].bitcast(E4), xr_scales[:], x_r[:].rearrange("p d t -> p (d t)"))
+
+        tsr_ps = bank("tsr_ps", "rot")
+        for b in range(BLOCKS):
+            turn(tsr_ps[:, b, :], ts_col[:, b : b + 1].to_broadcast([P, P]))
+        factor_planes = sb("factor_planes", [P, PACK, S], F32)
+        for t in range(PACK):
+            nc.scalar.activation(
+                factor_planes[:, t, :], tsr_ps[:].rearrange("p b s -> p (b s)"), ACT.Copy, scale=c_col[:, t : t + 1]
+            )
+        factor = sb("factor", [P, S, PACK], F32)
+        nc.scalar.copy(
+            factor[:].rearrange("p (c i) t -> p c t i", i=4),
+            factor_planes[:].rearrange("p t (c i) -> p c t i", i=4),
+        )
+
+        w_g = [sb("w_g%d" % h, [P, HALF, PACK], BF16) for h in range(2)]
+        w_codes = [sb("w_codes%d" % h, [P, HALF], U32) for h in range(2)]
+        w_scales = [sb("w_scales%d" % h, [P, HALF], U8) for h in range(2)]
+        for t in range(PACK):
+            for h in range(2):
+                listed = offsets[:, h * HALF // 16 : (h + 1) * HALF // 16]
+                nc.vector.tensor_copy(w_g[h][:, :, t], w_raw[t][:].indirect(listed))
+                if t == PACK - 1:
+                    nc.vector.quantize_mx(
+                        w_codes[h][:].bitcast(E4), w_scales[h][:], w_g[h][:].rearrange("p s t -> p (s t)")
+                    )
+
+        h_bf = sb("h_bf", [P, S, PACK], BF16)
+        h_codes = sb("h_codes", [P, S], U32)
+        h_scales = sb("h_scales", [P, S], U8)
+        nc.vector.memset(h_codes[:, HALF:S], 0)
+        nc.vector.memset(h_scales[:, HALF:S].bitcast(U32), 0)
+        resid = sb("resid", [P, S, PACK], F32)
+        y_woven = sb("y_woven", [P, S, PACK], F32)
+        probs = []
+        for b in range(BLOCKS):
+            half, cols_b = b // 2, slice((b % 2) * P, (b % 2 + 1) * P)
+            a_ps = bank("a_ps", "rot")
+            nc.tensor.matmul_mx(
+                a_ps[:].rearrange("p t m -> p (t m)"),
+                lhsT=w_codes[half][:, cols_b].bitcast(E4),
+                lhsT_scale=w_scales[half][:, cols_b],
+                rhs=xd_codes[:].bitcast(E4),
+                rhs_scale=xd_scales[:],
+                start=True,
+                stop=True,
+            )
+            scaled = sb("scaled%d" % b, [P, PACK, P], F32)
+            nc.vector.tensor_tensor(
+                scaled[:], a_ps[:].rearrange("p a b -> p (a b)").rearrange("p (m t) -> p t m", t=PACK), us_row[:], ALU.mult
+            )
+            prob = sb("prob%d" % b, [P, PACK, P], F32)
+            nc.scalar.activation(
+                prob[:], scaled[:], ACT.Sigmoid, bias=kb_col[:, b : b + 1], scale=ts_col[:, b : b + 1]
+            )
+            probs.append(prob)
+            slots = slice(b * P, (b + 1) * P)
+            nc.scalar.copy(
+                y_woven[:, slots, :].rearrange("p (c i) t -> p c t i", i=4),
+                y_raw[:, :, slots].rearrange("p t (c i) -> p c t i", i=4),
+            )
+
+        def product(t):
+            cols_t = slice(t * P, (t + 1) * P)
+            o_ps = bank("o_ps", "rot")
+            nc.tensor.matmul_mx(
+                o_ps[:].rearrange("p a b -> p (a b)"),
+                lhsT=xr_codes[:, cols_t].bitcast(E4),
+                lhsT_scale=xr_scales[:, cols_t],
+                rhs=h_codes[:].bitcast(E5),
+                rhs_scale=h_scales[:],
+                start=True,
+                stop=True,
+            )
+            return o_ps[:].rearrange("p a b -> p (a b)")
+
+        dw = [sb("dw%d" % t, [P, S], F32) for t in range(PACK)]
+        for half in range(2):
+            for b in (2 * half, 2 * half + 1):
+                slots = slice(b * P, (b + 1) * P)
+                p_ps = bank("p_ps", "held")
+                for t in range(PACK):
+                    turn(p_ps[:, t, :], probs[b][:, t, :])
+                nc.vector.tensor_tensor(
+                    resid[:, slots, :], p_ps[:].rearrange("m t s -> m s t"), y_woven[:, slots, :], ALU.subtract
+                )
+            for b in (2 * half, 2 * half + 1):
+                slots = slice(b * P, (b + 1) * P)
+                nc.vector.tensor_tensor(h_bf[:, slots, :], resid[:, slots, :], factor[:, slots, :], ALU.mult)
+            slots = slice(half * HALF, (half + 1) * HALF)
+            nc.vector.quantize_mx(
+                h_codes[:, slots].bitcast(E5), h_scales[:, slots], h_bf[:, slots, :].rearrange("p s t -> p (s t)")
+            )
+            if half == 0:
+                nc.scalar.copy(dw[0][:, 0:HALF], product(0)[:, 0:HALF])
+        nc.vector.tensor_copy(windows[0][:].indirect(offsets[:, 0 : HALF // 16]), dw[0][:, 0:HALF])
+
+        out_planes = out_0.rearrange("(p t) c -> t p c", t=PACK)
+        for t in range(PACK):
+            first = HALF if t == 0 else 0
+            nc.scalar.copy(dw[t][:, first:S], product(t)[:, first:S])
+            nc.vector.tensor_copy(windows[t][:].indirect(offsets[:, first // 16 : S // 16]), dw[t][:, first:S])
+            nc.sync.dma_start(out_planes[t], windows[t][:])
+
+        g = sb("g", [P, PACK, S], F32, tag="dw0")
+        for t in range(PACK):
+            nc.scalar.activation(g[:, t, :], resid[:, :, t], ACT.Copy, scale=wt_col[:, t : t + 1])
+        sum_ps = bank("sum_ps", "rot")
+        for b in range(BLOCKS):
+            for t in range(PACK):
+                turn(sum_ps[:, b, :], g[:, t, b * P : (b + 1) * P], start=(t == 0), stop=(t == PACK - 1))
+        db_col = sb("db_col", [P, BLOCKS], F32)
+        spare = sb("spare", [P, P], F32)
+        for b in range(BLOCKS):
+            nc.scalar.activation(spare[:], sum_ps[:, b, :], ACT.Copy, accum_out=db_col[:, b : b + 1])
+        row_ps = bank("row_ps", "rot")
+        for b in range(BLOCKS):
+            turn(row_ps[:, b, :], db_col[:, b : b + 1].to_broadcast([P, P]))
+        db_row = sb("db_row", [1, S], F32)
+        nc.scalar.copy(db_row[:], row_ps[0:1, :, :].rearrange("p a b -> p (a b)"))
+        nc.scalar.dma_start(out_1, db_row[:])

@@ -11,6 +11,7 @@ BYTES = 4 * (D * R + D * T + 2 * T + 2 * R + R * S + D * T + S) + 2 * P * (S // 
 
 F32 = mybir.dt.float32
 BF16 = mybir.dt.bfloat16
+I32 = mybir.dt.int32
 U32 = mybir.dt.uint32
 U16 = mybir.dt.uint16
 U8 = mybir.dt.uint8
@@ -34,7 +35,7 @@ def tile_attend_gbias_wb_log_kernel(tc, xT, wT, ts, kb, us, y, wt, offs, out_0, 
             return keep.tile(shape, dtype, name=name, tag=tag or name, align_bytes=64)
 
         def bank(name, tag):
-            return psum.tile([P, PACK, P], F32, name=name, tag=tag)
+            return psum.tile([P, PACK, P], F32, name=name, tag=tag, bufs=(4 if tag == "held" else 3))
 
         def turn(out, in_, start=True, stop=True):
             nc.tensor.matmul(out, in_, ident[:], start=start, stop=stop, is_transpose=True)
@@ -64,12 +65,8 @@ def tile_attend_gbias_wb_log_kernel(tc, xT, wT, ts, kb, us, y, wt, offs, out_0, 
         warm = sb("warm", [P, 1], F32)
         nc.scalar.activation(warm[:], ident[:, 0:1], ACT.Sigmoid)
 
-        nc.vector.memset(ts_win[0:ROW, :], 0.0)
-        nc.vector.memset(kb_win[0:ROW, :], 0.0)
-        windows = [sb("window%d" % t, [P, T], F32) for t in range(PACK)]
-        for t in range(PACK):
-            for c0 in range(0, T, 1024):
-                nc.gpsimd.memset(windows[t][:, c0 : c0 + 1024], 0.0)
+        nc.vector.memset(ts_win[0:ROW, :].bitcast(I32), 0)
+        nc.vector.memset(kb_win[0:ROW, :].bitcast(I32), 0)
 
         us_ps = bank("us_ps", "rot")
         for t in range(PACK):
@@ -91,6 +88,11 @@ def tile_attend_gbias_wb_log_kernel(tc, xT, wT, ts, kb, us, y, wt, offs, out_0, 
             cols.append(col)
         ts_col, kb_col = cols
 
+        window_0 = sb("window_0", [P, T], F32)
+        nc.vector.memset(window_0[:].bitcast(I32), 0)
+        window_2 = sb("window_2", [P, T], F32)
+        nc.vector.memset(window_2[:].bitcast(I32), 0)
+
         x_d = sb("x_d", [P, R, PACK], BF16)
         nc.scalar.copy(
             x_d[:].rearrange("p (c i) t -> p c t i", i=4),
@@ -110,19 +112,9 @@ def tile_attend_gbias_wb_log_kernel(tc, xT, wT, ts, kb, us, y, wt, offs, out_0, 
         xr_scales = sb("xr_scales", [P, D], U8)
         nc.vector.quantize_mx(xr_codes[:].bitcast(E4), xr_scales[:], x_r[:].rearrange("p d t -> p (d t)"))
 
-        tsr_ps = bank("tsr_ps", "rot")
+        tsr_ps = psum.tile([P, S], F32, name="tsr_ps", tag="tsr", bufs=1)
         for b in range(BLOCKS):
-            turn(tsr_ps[:, b, :], ts_col[:, b : b + 1].to_broadcast([P, P]))
-        factor_planes = sb("factor_planes", [P, PACK, S], F32)
-        for t in range(PACK):
-            nc.scalar.activation(
-                factor_planes[:, t, :], tsr_ps[:].rearrange("p b s -> p (b s)"), ACT.Copy, scale=c_col[:, t : t + 1]
-            )
-        factor = sb("factor", [P, S, PACK], F32)
-        nc.scalar.copy(
-            factor[:].rearrange("p (c i) t -> p c t i", i=4),
-            factor_planes[:].rearrange("p t (c i) -> p c t i", i=4),
-        )
+            turn(tsr_ps[:, b * P : (b + 1) * P], ts_col[:, b : b + 1].to_broadcast([P, P]))
 
         w_g = [sb("w_g%d" % h, [P, HALF, PACK], BF16) for h in range(2)]
         w_codes = [sb("w_codes%d" % h, [P, HALF], U32) for h in range(2)]
@@ -136,13 +128,12 @@ def tile_attend_gbias_wb_log_kernel(tc, xT, wT, ts, kb, us, y, wt, offs, out_0, 
                         w_codes[h][:].bitcast(E4), w_scales[h][:], w_g[h][:].rearrange("p s t -> p (s t)")
                     )
 
-        h_bf = sb("h_bf", [P, S, PACK], BF16)
+
         h_codes = sb("h_codes", [P, S], U32)
         h_scales = sb("h_scales", [P, S], U8)
         nc.vector.memset(h_codes[:, HALF:S], 0)
         nc.vector.memset(h_scales[:, HALF:S].bitcast(U32), 0)
-        resid = sb("resid", [P, S, PACK], F32)
-        y_woven = sb("y_woven", [P, S, PACK], F32)
+        resid = sb("resid", [P, PACK, S], F32)
         probs = []
         for b in range(BLOCKS):
             half, cols_b = b // 2, slice((b % 2) * P, (b % 2 + 1) * P)
@@ -165,11 +156,6 @@ def tile_attend_gbias_wb_log_kernel(tc, xT, wT, ts, kb, us, y, wt, offs, out_0, 
                 prob[:], scaled[:], ACT.Sigmoid, bias=kb_col[:, b : b + 1], scale=ts_col[:, b : b + 1]
             )
             probs.append(prob)
-            slots = slice(b * P, (b + 1) * P)
-            nc.scalar.copy(
-                y_woven[:, slots, :].rearrange("p (c i) t -> p c t i", i=4),
-                y_raw[:, :, slots].rearrange("p t (c i) -> p c t i", i=4),
-            )
 
         def product(t):
             cols_t = slice(t * P, (t + 1) * P)
@@ -185,26 +171,44 @@ def tile_attend_gbias_wb_log_kernel(tc, xT, wT, ts, kb, us, y, wt, offs, out_0, 
             )
             return o_ps[:].rearrange("p a b -> p (a b)")
 
-        dw = [sb("dw%d" % t, [P, S], F32) for t in range(PACK)]
-        for half in range(2):
+        def residuals(half):
             for b in (2 * half, 2 * half + 1):
                 slots = slice(b * P, (b + 1) * P)
                 p_ps = bank("p_ps", "held")
                 for t in range(PACK):
                     turn(p_ps[:, t, :], probs[b][:, t, :])
-                nc.vector.tensor_tensor(
-                    resid[:, slots, :], p_ps[:].rearrange("m t s -> m s t"), y_woven[:, slots, :], ALU.subtract
-                )
-            for b in (2 * half, 2 * half + 1):
-                slots = slice(b * P, (b + 1) * P)
-                nc.vector.tensor_tensor(h_bf[:, slots, :], resid[:, slots, :], factor[:, slots, :], ALU.mult)
+                nc.vector.tensor_tensor(resid[:, :, slots], p_ps[:], y_raw[:, :, slots], ALU.subtract)
+
+        def weighted(half):
             slots = slice(half * HALF, (half + 1) * HALF)
-            nc.vector.quantize_mx(
-                h_codes[:, slots].bitcast(E5), h_scales[:, slots], h_bf[:, slots, :].rearrange("p s t -> p (s t)")
+            planes = sb("h_planes%d" % half, [P, PACK, HALF], BF16, tag=("h_woven0" if half else None))
+            for t in range(PACK):
+                nc.vector.scalar_tensor_tensor(
+                    planes[:, t, :], resid[:, t, slots], c_col[:, t : t + 1], tsr_ps[:, slots], ALU.mult, ALU.mult
+                )
+            woven = sb("h_woven%d" % half, [P, HALF, PACK], BF16)
+            nc.scalar.copy(
+                woven[:].rearrange("p (c i) t -> p c t i", i=4),
+                planes[:].rearrange("p t (c i) -> p c t i", i=4),
             )
-            if half == 0:
-                nc.scalar.copy(dw[0][:, 0:HALF], product(0)[:, 0:HALF])
-        nc.vector.tensor_copy(windows[0][:].indirect(offsets[:, 0 : HALF // 16]), dw[0][:, 0:HALF])
+            return woven
+
+        def quantize_h(half, woven):
+            slots = slice(half * HALF, (half + 1) * HALF)
+            nc.vector.quantize_mx(h_codes[:, slots].bitcast(E5), h_scales[:, slots], woven[:].rearrange("p s t -> p (s t)"))
+
+        dw = [sb("dw%d" % t, [P, S], F32) for t in range(PACK)]
+        residuals(0)
+        woven_0 = weighted(0)
+        residuals(1)
+        quantize_h(0, woven_0)
+        nc.scalar.copy(dw[0][:, 0:HALF], product(0)[:, 0:HALF])
+        woven_1 = weighted(1)
+        nc.vector.tensor_copy(window_0[:].indirect(offsets[:, 0 : HALF // 16]), dw[0][:, 0:HALF])
+        quantize_h(1, woven_1)
+        window_1 = sb("window_1", [P, T], F32, tag="h_woven1")
+        nc.vector.memset(window_1[:].bitcast(I32), 0)
+        windows = [window_0, window_1, window_2, window_0]
 
         out_planes = out_0.rearrange("(p t) c -> t p c", t=PACK)
         for t in range(PACK):
@@ -213,9 +217,9 @@ def tile_attend_gbias_wb_log_kernel(tc, xT, wT, ts, kb, us, y, wt, offs, out_0, 
             nc.vector.tensor_copy(windows[t][:].indirect(offsets[:, first // 16 : S // 16]), dw[t][:, first:S])
             nc.sync.dma_start(out_planes[t], windows[t][:])
 
-        g = sb("g", [P, PACK, S], F32, tag="dw0")
+        g = sb("g", [P, PACK, S], F32, tag="xr_codes")
         for t in range(PACK):
-            nc.scalar.activation(g[:, t, :], resid[:, :, t], ACT.Copy, scale=wt_col[:, t : t + 1])
+            nc.scalar.activation(g[:, t, :], resid[:, t, :], ACT.Copy, scale=wt_col[:, t : t + 1])
         sum_ps = bank("sum_ps", "rot")
         for b in range(BLOCKS):
             for t in range(PACK):

@@ -35,7 +35,7 @@ def tile_attend_gbias_wb_log_kernel(tc, xT, wT, ts, kb, us, y, wt, offs, out_0, 
             return keep.tile(shape, dtype, name=name, tag=tag or name, align_bytes=64)
 
         def bank(name, tag):
-            return psum.tile([P, PACK, P], F32, name=name, tag=tag, bufs=(4 if tag == "held" else 3))
+            return psum.tile([P, PACK, P], F32, name=name, tag=tag, bufs=(3 if tag == "held" else 4))
 
         def turn(out, in_, start=True, stop=True):
             nc.tensor.matmul(out, in_, ident[:], start=start, stop=stop, is_transpose=True)
@@ -90,27 +90,23 @@ def tile_attend_gbias_wb_log_kernel(tc, xT, wT, ts, kb, us, y, wt, offs, out_0, 
 
         window_0 = sb("window_0", [P, T], F32)
         nc.vector.memset(window_0[:].bitcast(I32), 0)
-        window_2 = sb("window_2", [P, T], F32)
-        nc.vector.memset(window_2[:].bitcast(I32), 0)
 
         x_d = sb("x_d", [P, R, PACK], BF16)
         nc.scalar.copy(
             x_d[:].rearrange("p (c i) t -> p c t i", i=4),
             x_raw[:].rearrange("p t (c i) -> p c t i", i=4),
         )
-        xd_codes = sb("xd_codes", [P, R], U32)
-        xd_scales = sb("xd_scales", [P, R], U8)
-        nc.vector.quantize_mx(xd_codes[:].bitcast(E4), xd_scales[:], x_d[:].rearrange("p r t -> p (r t)"))
 
         x_r = sb("x_r", [P, D, PACK], BF16)
-        for t in range(PACK):
+        x_words = x_d[:].rearrange("p r t -> p (r t)").bitcast(F32)
+        for u in range(2):
             xt_ps = bank("xt_ps", "held")
             for j in range(PACK):
-                turn(xt_ps[:, j, :], x_raw[:, t, j:R:PACK])
-            nc.scalar.copy(x_r[:, t * P : (t + 1) * P, :], xt_ps[:].rearrange("m j p -> m p j"))
-        xr_codes = sb("xr_codes", [P, D], U32)
-        xr_scales = sb("xr_scales", [P, D], U8)
-        nc.vector.quantize_mx(xr_codes[:].bitcast(E4), xr_scales[:], x_r[:].rearrange("p d t -> p (d t)"))
+                turn(xt_ps[:, j, :], x_words[:, 2 * j + u : 2 * R : 2 * PACK])
+            nc.scalar.copy(
+                x_r[:, 2 * u * P : 2 * (u + 1) * P, :].rearrange("m (e p) j -> m e p j", e=2),
+                xt_ps[:].rearrange("m j p -> m (j p)").bitcast(BF16).rearrange("m (j p e) -> m e p j", j=PACK, e=2),
+            )
 
         tsr_ps = psum.tile([P, S], F32, name="tsr_ps", tag="tsr", bufs=1)
         for b in range(BLOCKS):
@@ -119,15 +115,26 @@ def tile_attend_gbias_wb_log_kernel(tc, xT, wT, ts, kb, us, y, wt, offs, out_0, 
         w_g = [sb("w_g%d" % h, [P, HALF, PACK], BF16) for h in range(2)]
         w_codes = [sb("w_codes%d" % h, [P, HALF], U32) for h in range(2)]
         w_scales = [sb("w_scales%d" % h, [P, HALF], U8) for h in range(2)]
-        for t in range(PACK):
-            for h in range(2):
-                listed = offsets[:, h * HALF // 16 : (h + 1) * HALF // 16]
-                nc.vector.tensor_copy(w_g[h][:, :, t], w_raw[t][:].indirect(listed))
-                if t == PACK - 1:
-                    nc.vector.quantize_mx(
-                        w_codes[h][:].bitcast(E4), w_scales[h][:], w_g[h][:].rearrange("p s t -> p (s t)")
-                    )
-
+        w_picked = sb("w_picked", [P, PACK, S], BF16)
+        for t in range(PACK - 1):
+            nc.vector.tensor_copy(w_picked[:, t, :], w_raw[t][:].indirect(offsets[:]))
+            if t == 0:
+                xd_codes = sb("xd_codes", [P, R], U32, tag="w_raw0")
+                xd_scales = sb("xd_scales", [P, R], U8)
+                nc.vector.quantize_mx(xd_codes[:].bitcast(E4), xd_scales[:], x_d[:].rearrange("p r t -> p (r t)"))
+        for h, weave in enumerate((nc.scalar.copy, nc.vector.tensor_copy)):
+            slots = slice(h * HALF, (h + 1) * HALF)
+            listed = offsets[:, h * HALF // 16 : (h + 1) * HALF // 16]
+            nc.vector.tensor_copy(w_picked[:, PACK - 1, slots], w_raw[PACK - 1][:].indirect(listed))
+            weave(
+                w_g[h][:].rearrange("p (c i) t -> p c t i", i=4),
+                w_picked[:, :, slots].rearrange("p t (c i) -> p c t i", i=4),
+            )
+        for h in range(2):
+            nc.vector.quantize_mx(w_codes[h][:].bitcast(E4), w_scales[h][:], w_g[h][:].rearrange("p s t -> p (s t)"))
+        xr_codes = sb("xr_codes", [P, D], U32, tag="w_g1")
+        xr_scales = sb("xr_scales", [P, D], U8)
+        nc.vector.quantize_mx(xr_codes[:].bitcast(E4), xr_scales[:], x_r[:].rearrange("p d t -> p (d t)"))
 
         h_codes = sb("h_codes", [P, S], U32)
         h_scales = sb("h_scales", [P, S], U8)
@@ -201,6 +208,8 @@ def tile_attend_gbias_wb_log_kernel(tc, xT, wT, ts, kb, us, y, wt, offs, out_0, 
         residuals(0)
         woven_0 = weighted(0)
         residuals(1)
+        window_2 = sb("window_2", [P, T], F32, tag="y_raw")
+        nc.vector.memset(window_2[:].bitcast(I32), 0)
         quantize_h(0, woven_0)
         nc.scalar.copy(dw[0][:, 0:HALF], product(0)[:, 0:HALF])
         woven_1 = weighted(1)
@@ -217,7 +226,7 @@ def tile_attend_gbias_wb_log_kernel(tc, xT, wT, ts, kb, us, y, wt, offs, out_0, 
             nc.vector.tensor_copy(windows[t][:].indirect(offsets[:, first // 16 : S // 16]), dw[t][:, first:S])
             nc.sync.dma_start(out_planes[t], windows[t][:])
 
-        g = sb("g", [P, PACK, S], F32, tag="xr_codes")
+        g = sb("g", [P, PACK, S], F32, tag="w_g1")
         for t in range(PACK):
             nc.scalar.activation(g[:, t, :], resid[:, t, :], ACT.Copy, scale=wt_col[:, t : t + 1])
         sum_ps = bank("sum_ps", "rot")

@@ -22,7 +22,10 @@ ALU = mybir.AluOpType
 
 HALF = S // 2
 BLOCKS = S // P
-ROW = P - 1
+PER_COLUMN = 16
+LINE = 4
+LOADED = P - 1
+BANKS = {"turned": 3, "product": 4}
 
 
 def tile_attend_gbias_wb_log_kernel(tc, xT, wT, ts, kb, us, y, wt, offs, out_0, out_1):
@@ -35,24 +38,36 @@ def tile_attend_gbias_wb_log_kernel(tc, xT, wT, ts, kb, us, y, wt, offs, out_0, 
             return keep.tile(shape, dtype, name=name, tag=tag or name, align_bytes=64)
 
         def bank(name, tag):
-            return psum.tile([P, PACK, P], F32, name=name, tag=tag, bufs=(3 if tag == "held" else 4))
+            return psum.tile([P, PACK, P], F32, name=name, tag=tag, bufs=BANKS[tag])
+
+        def flat(tile):
+            return tile[:].rearrange("p a b -> p (a b)")
 
         def turn(out, in_, start=True, stop=True):
             nc.tensor.matmul(out, in_, ident[:], start=start, stop=stop, is_transpose=True)
 
-        offsets = keep.tile([P, S // 16], U16, name="offsets")
+        def spread(out, column):
+            turn(out, column.to_broadcast([P, P]))
+
+        def weave(woven, planes):
+            nc.scalar.copy(
+                woven.rearrange("p (c i) t -> p c t i", i=LINE),
+                planes.rearrange("p t (c i) -> p c t i", i=LINE),
+            )
+
+        offsets = keep.tile([P, S // PER_COLUMN], U16, name="offsets")
         x_raw = sb("x_raw", [P, PACK, R], F32)
         y_raw = sb("y_raw", [P, PACK, S], F32)
         w_raw = [sb("w_raw%d" % t, [P, T], F32) for t in range(PACK)]
-        ts_win = sb("ts_win", [P, T], F32)
-        kb_win = sb("kb_win", [P, T], F32)
+        ts_table = sb("ts_table", [P, T], F32)
+        kb_table = sb("kb_table", [P, T], F32)
         us_col = sb("us_col", [P, PACK], F32)
         wt_col = sb("wt_col", [P, PACK], F32)
 
         nc.sync.dma_start(x_raw[:], xT.rearrange("(p t) r -> p t r", t=PACK))
         nc.sync.dma_start(offsets[:], offs)
-        nc.scalar.dma_start(ts_win[ROW:P, :], ts[0:1, :])
-        nc.scalar.dma_start(kb_win[ROW:P, :], kb[0:1, :])
+        nc.scalar.dma_start(ts_table[LOADED:P, :], ts[0:1, :])
+        nc.scalar.dma_start(kb_table[LOADED:P, :], kb[0:1, :])
         nc.sync.dma_start(us_col[:], us.rearrange("(p t) o -> p (t o)", t=PACK))
         nc.sync.dma_start(wt_col[:], wt.rearrange("(p t) o -> p (t o)", t=PACK))
         w_planes = wT.rearrange("(p t) c -> t p c", t=PACK)
@@ -62,184 +77,162 @@ def tile_attend_gbias_wb_log_kernel(tc, xT, wT, ts, kb, us, y, wt, offs, out_0, 
 
         ident = sb("ident", [P, P], F32)
         make_identity(nc, ident[:])
-        warm = sb("warm", [P, 1], F32)
-        nc.scalar.activation(warm[:], ident[:, 0:1], ACT.Sigmoid)
 
-        nc.vector.memset(ts_win[0:ROW, :].bitcast(I32), 0)
-        nc.vector.memset(kb_win[0:ROW, :].bitcast(I32), 0)
+        nc.vector.memset(ts_table[0:LOADED, :].bitcast(I32), 0)
+        nc.vector.memset(kb_table[0:LOADED, :].bitcast(I32), 0)
 
-        us_ps = bank("us_ps", "rot")
+        us_ps = bank("us_ps", "product")
         for t in range(PACK):
-            turn(us_ps[:, t, :], us_col[:, t : t + 1].to_broadcast([P, P]))
+            spread(us_ps[:, t, :], us_col[:, t : t + 1])
         us_row = sb("us_row", [P, PACK, P], F32)
         nc.scalar.copy(us_row[:], us_ps[:])
-        c_col = sb("c_col", [P, PACK], F32)
-        nc.vector.tensor_tensor(c_col[:], us_col[:], wt_col[:], ALU.mult)
+        us_wt_col = sb("us_wt_col", [P, PACK], F32)
+        nc.vector.tensor_tensor(us_wt_col[:], us_col[:], wt_col[:], ALU.mult)
 
-        cols = []
-        for name, win in (("ts", ts_win), ("kb", kb_win)):
+        listed_cols = []
+        for name, table in (("ts", ts_table), ("kb", kb_table)):
             picked = sb(name + "_picked", [P, S], F32)
-            nc.vector.tensor_copy(picked[:], win[:].indirect(offsets[:]))
-            col_ps = bank(name + "_ps", "rot")
+            nc.vector.tensor_copy(picked[:], table[:].indirect(offsets[:]))
+            col_ps = bank(name + "_ps", "product")
             for b in range(BLOCKS):
                 turn(col_ps[:, b, :], picked[:, b * P : (b + 1) * P])
             col = sb(name + "_col", [P, BLOCKS], F32)
-            nc.scalar.copy(col[:], col_ps[:, :, ROW])
-            cols.append(col)
-        ts_col, kb_col = cols
+            nc.scalar.copy(col[:], col_ps[:, :, LOADED])
+            listed_cols.append(col)
+        ts_col, kb_col = listed_cols
 
         window_0 = sb("window_0", [P, T], F32)
         nc.vector.memset(window_0[:].bitcast(I32), 0)
+        window_2 = sb("window_2", [P, T], F32)
+        nc.vector.memset(window_2[:].bitcast(I32), 0)
 
         x_d = sb("x_d", [P, R, PACK], BF16)
-        nc.scalar.copy(
-            x_d[:].rearrange("p (c i) t -> p c t i", i=4),
-            x_raw[:].rearrange("p t (c i) -> p c t i", i=4),
-        )
+        weave(x_d[:], x_raw[:])
 
         x_r = sb("x_r", [P, D, PACK], BF16)
-        x_words = x_d[:].rearrange("p r t -> p (r t)").bitcast(F32)
+        x_words = flat(x_d).bitcast(F32)
         for u in range(2):
-            xt_ps = bank("xt_ps", "held")
+            xt_ps = bank("xt_ps", "turned")
             for j in range(PACK):
                 turn(xt_ps[:, j, :], x_words[:, 2 * j + u : 2 * R : 2 * PACK])
             nc.scalar.copy(
                 x_r[:, 2 * u * P : 2 * (u + 1) * P, :].rearrange("m (e p) j -> m e p j", e=2),
-                xt_ps[:].rearrange("m j p -> m (j p)").bitcast(BF16).rearrange("m (j p e) -> m e p j", j=PACK, e=2),
+                flat(xt_ps).bitcast(BF16).rearrange("m (j p e) -> m e p j", j=PACK, e=2),
             )
 
-        tsr_ps = psum.tile([P, S], F32, name="tsr_ps", tag="tsr", bufs=1)
+        ts_row_ps = psum.tile([P, S], F32, name="ts_row_ps", tag="ts_row", bufs=1)
         for b in range(BLOCKS):
-            turn(tsr_ps[:, b * P : (b + 1) * P], ts_col[:, b : b + 1].to_broadcast([P, P]))
+            spread(ts_row_ps[:, b * P : (b + 1) * P], ts_col[:, b : b + 1])
+        factor_planes = sb("factor_planes", [P, PACK, S], F32)
+        for t in range(PACK):
+            nc.scalar.activation(factor_planes[:, t, :], ts_row_ps[:], ACT.Copy, scale=us_wt_col[:, t : t + 1])
+        factor = sb("factor", [P, S, PACK], F32)
+        weave(factor[:], factor_planes[:])
 
-        w_g = [sb("w_g%d" % h, [P, HALF, PACK], BF16) for h in range(2)]
-        w_codes = [sb("w_codes%d" % h, [P, HALF], U32) for h in range(2)]
-        w_scales = [sb("w_scales%d" % h, [P, HALF], U8) for h in range(2)]
-        w_picked = sb("w_picked", [P, PACK, S], BF16)
-        for t in range(PACK - 1):
-            nc.vector.tensor_copy(w_picked[:, t, :], w_raw[t][:].indirect(offsets[:]))
-            if t == 0:
-                xd_codes = sb("xd_codes", [P, R], U32, tag="w_raw0")
-                xd_scales = sb("xd_scales", [P, R], U8)
-                nc.vector.quantize_mx(xd_codes[:].bitcast(E4), xd_scales[:], x_d[:].rearrange("p r t -> p (r t)"))
-        for h, weave in enumerate((nc.scalar.copy, nc.vector.tensor_copy)):
-            slots = slice(h * HALF, (h + 1) * HALF)
-            listed = offsets[:, h * HALF // 16 : (h + 1) * HALF // 16]
-            nc.vector.tensor_copy(w_picked[:, PACK - 1, slots], w_raw[PACK - 1][:].indirect(listed))
-            weave(
-                w_g[h][:].rearrange("p (c i) t -> p c t i", i=4),
-                w_picked[:, :, slots].rearrange("p t (c i) -> p c t i", i=4),
-            )
-        for h in range(2):
-            nc.vector.quantize_mx(w_codes[h][:].bitcast(E4), w_scales[h][:], w_g[h][:].rearrange("p s t -> p (s t)"))
-        xr_codes = sb("xr_codes", [P, D], U32, tag="w_g1")
-        xr_scales = sb("xr_scales", [P, D], U8)
-        nc.vector.quantize_mx(xr_codes[:].bitcast(E4), xr_scales[:], x_r[:].rearrange("p d t -> p (d t)"))
+        w_woven = [sb("w_woven%d" % half, [P, HALF, PACK], BF16) for half in range(2)]
+        w_codes = [sb("w_codes%d" % half, [P, HALF], U32) for half in range(2)]
+        w_scales = [sb("w_scales%d" % half, [P, HALF], U8) for half in range(2)]
 
+        def gather_w(t, half):
+            listed = offsets[:, half * HALF // PER_COLUMN : (half + 1) * HALF // PER_COLUMN]
+            nc.vector.tensor_copy(w_woven[half][:, :, t], w_raw[t][:].indirect(listed))
+
+        def quantize_x(name, woven, tag):
+            codes = sb(name + "_codes", [P, woven.shape[1]], U32, tag=tag)
+            scales = sb(name + "_scales", [P, woven.shape[1]], U8)
+            nc.vector.quantize_mx(codes[:].bitcast(E4), scales[:], flat(woven))
+            return codes, scales
+
+        gather_w(0, 0)
+        gather_w(0, 1)
+        xd_codes, xd_scales = quantize_x("xd", x_d, "w_raw0")
+        for t in (1, 2):
+            gather_w(t, 0)
+            gather_w(t, 1)
+        xr_codes, xr_scales = quantize_x("xr", x_r, "w_raw2")
+        for half in range(2):
+            gather_w(PACK - 1, half)
+            nc.vector.quantize_mx(w_codes[half][:].bitcast(E4), w_scales[half][:], flat(w_woven[half]))
+
+        h_woven = [sb("h_woven%d" % half, [P, HALF, PACK], BF16) for half in range(2)]
         h_codes = sb("h_codes", [P, S], U32)
         h_scales = sb("h_scales", [P, S], U8)
-        nc.vector.memset(h_codes[:, HALF:S], 0)
-        nc.vector.memset(h_scales[:, HALF:S].bitcast(U32), 0)
-        resid = sb("resid", [P, PACK, S], F32)
+        resid = sb("resid", [P, S, PACK], F32)
+        y_woven = sb("y_woven", [P, S, PACK], F32)
         probs = []
         for b in range(BLOCKS):
-            half, cols_b = b // 2, slice((b % 2) * P, (b % 2 + 1) * P)
-            a_ps = bank("a_ps", "rot")
+            half, within = b // 2, slice((b % 2) * P, (b % 2 + 1) * P)
+            a_ps = bank("a_ps", "product")
             nc.tensor.matmul_mx(
-                a_ps[:].rearrange("p t m -> p (t m)"),
-                lhsT=w_codes[half][:, cols_b].bitcast(E4),
-                lhsT_scale=w_scales[half][:, cols_b],
+                flat(a_ps),
+                lhsT=w_codes[half][:, within].bitcast(E4),
+                lhsT_scale=w_scales[half][:, within],
                 rhs=xd_codes[:].bitcast(E4),
                 rhs_scale=xd_scales[:],
                 start=True,
                 stop=True,
             )
             scaled = sb("scaled%d" % b, [P, PACK, P], F32)
-            nc.vector.tensor_tensor(
-                scaled[:], a_ps[:].rearrange("p a b -> p (a b)").rearrange("p (m t) -> p t m", t=PACK), us_row[:], ALU.mult
-            )
+            nc.vector.tensor_tensor(scaled[:], flat(a_ps).rearrange("p (m t) -> p t m", t=PACK), us_row[:], ALU.mult)
             prob = sb("prob%d" % b, [P, PACK, P], F32)
-            nc.scalar.activation(
-                prob[:], scaled[:], ACT.Sigmoid, bias=kb_col[:, b : b + 1], scale=ts_col[:, b : b + 1]
-            )
+            nc.scalar.activation(prob[:], scaled[:], ACT.Sigmoid, bias=kb_col[:, b : b + 1], scale=ts_col[:, b : b + 1])
             probs.append(prob)
+            slots = slice(b * P, (b + 1) * P)
+            weave(y_woven[:, slots, :], y_raw[:, :, slots])
 
-        def product(t):
-            cols_t = slice(t * P, (t + 1) * P)
-            o_ps = bank("o_ps", "rot")
-            nc.tensor.matmul_mx(
-                o_ps[:].rearrange("p a b -> p (a b)"),
-                lhsT=xr_codes[:, cols_t].bitcast(E4),
-                lhsT_scale=xr_scales[:, cols_t],
-                rhs=h_codes[:].bitcast(E5),
-                rhs_scale=h_scales[:],
-                start=True,
-                stop=True,
-            )
-            return o_ps[:].rearrange("p a b -> p (a b)")
-
-        def residuals(half):
-            for b in (2 * half, 2 * half + 1):
+        for half in range(2):
+            blocks = (2 * half, 2 * half + 1)
+            for b in blocks:
                 slots = slice(b * P, (b + 1) * P)
-                p_ps = bank("p_ps", "held")
+                p_ps = bank("p_ps", "turned")
                 for t in range(PACK):
                     turn(p_ps[:, t, :], probs[b][:, t, :])
-                nc.vector.tensor_tensor(resid[:, :, slots], p_ps[:], y_raw[:, :, slots], ALU.subtract)
-
-        def weighted(half):
-            slots = slice(half * HALF, (half + 1) * HALF)
-            planes = sb("h_planes%d" % half, [P, PACK, HALF], BF16, tag=("h_woven0" if half else None))
-            for t in range(PACK):
-                nc.vector.scalar_tensor_tensor(
-                    planes[:, t, :], resid[:, t, slots], c_col[:, t : t + 1], tsr_ps[:, slots], ALU.mult, ALU.mult
+                nc.vector.tensor_tensor(
+                    resid[:, slots, :], p_ps[:].rearrange("m t s -> m s t"), y_woven[:, slots, :], ALU.subtract
                 )
-            woven = sb("h_woven%d" % half, [P, HALF, PACK], BF16)
-            nc.scalar.copy(
-                woven[:].rearrange("p (c i) t -> p c t i", i=4),
-                planes[:].rearrange("p t (c i) -> p c t i", i=4),
-            )
-            return woven
-
-        def quantize_h(half, woven):
+            for b in blocks:
+                slots, within = slice(b * P, (b + 1) * P), slice((b % 2) * P, (b % 2 + 1) * P)
+                nc.vector.tensor_tensor(h_woven[half][:, within, :], resid[:, slots, :], factor[:, slots, :], ALU.mult)
             slots = slice(half * HALF, (half + 1) * HALF)
-            nc.vector.quantize_mx(h_codes[:, slots].bitcast(E5), h_scales[:, slots], woven[:].rearrange("p s t -> p (s t)"))
+            nc.vector.quantize_mx(h_codes[:, slots].bitcast(E5), h_scales[:, slots], flat(h_woven[half]))
 
-        dw = [sb("dw%d" % t, [P, S], F32) for t in range(PACK)]
-        residuals(0)
-        woven_0 = weighted(0)
-        residuals(1)
-        window_2 = sb("window_2", [P, T], F32, tag="y_raw")
-        nc.vector.memset(window_2[:].bitcast(I32), 0)
-        quantize_h(0, woven_0)
-        nc.scalar.copy(dw[0][:, 0:HALF], product(0)[:, 0:HALF])
-        woven_1 = weighted(1)
-        nc.vector.tensor_copy(window_0[:].indirect(offsets[:, 0 : HALF // 16]), dw[0][:, 0:HALF])
-        quantize_h(1, woven_1)
         window_1 = sb("window_1", [P, T], F32, tag="h_woven1")
         nc.vector.memset(window_1[:].bitcast(I32), 0)
         windows = [window_0, window_1, window_2, window_0]
 
         out_planes = out_0.rearrange("(p t) c -> t p c", t=PACK)
         for t in range(PACK):
-            first = HALF if t == 0 else 0
-            nc.scalar.copy(dw[t][:, first:S], product(t)[:, first:S])
-            nc.vector.tensor_copy(windows[t][:].indirect(offsets[:, first // 16 : S // 16]), dw[t][:, first:S])
-            nc.sync.dma_start(out_planes[t], windows[t][:])
+            dw = sb("dw%d" % t, [P, S], F32)
+            features = slice(t * P, (t + 1) * P)
+            o_ps = bank("o_ps", "product")
+            nc.tensor.matmul_mx(
+                flat(o_ps),
+                lhsT=xr_codes[:, features].bitcast(E4),
+                lhsT_scale=xr_scales[:, features],
+                rhs=h_codes[:].bitcast(E5),
+                rhs_scale=h_scales[:],
+                start=True,
+                stop=True,
+            )
+            nc.scalar.copy(dw[:], flat(o_ps))
+            nc.vector.tensor_copy(windows[t][:].indirect(offsets[:]), dw[:])
+            queue = nc.scalar if t == PACK - 1 else nc.sync
+            queue.dma_start(out_planes[t], windows[t][:])
 
-        g = sb("g", [P, PACK, S], F32, tag="w_g1")
+        g = sb("g", [P, PACK, S], F32, tag="w_raw2")
         for t in range(PACK):
-            nc.scalar.activation(g[:, t, :], resid[:, t, :], ACT.Copy, scale=wt_col[:, t : t + 1])
-        sum_ps = bank("sum_ps", "rot")
+            nc.scalar.activation(g[:, t, :], resid[:, :, t], ACT.Copy, scale=wt_col[:, t : t + 1])
+        sum_ps = bank("sum_ps", "product")
         for b in range(BLOCKS):
             for t in range(PACK):
                 turn(sum_ps[:, b, :], g[:, t, b * P : (b + 1) * P], start=(t == 0), stop=(t == PACK - 1))
         db_col = sb("db_col", [P, BLOCKS], F32)
-        spare = sb("spare", [P, P], F32)
+        copied = sb("copied", [P, P], F32)
         for b in range(BLOCKS):
-            nc.scalar.activation(spare[:], sum_ps[:, b, :], ACT.Copy, accum_out=db_col[:, b : b + 1])
-        row_ps = bank("row_ps", "rot")
+            nc.scalar.activation(copied[:], sum_ps[:, b, :], ACT.Copy, accum_out=db_col[:, b : b + 1])
+        row_ps = bank("row_ps", "product")
         for b in range(BLOCKS):
-            turn(row_ps[:, b, :], db_col[:, b : b + 1].to_broadcast([P, P]))
+            spread(row_ps[:, b, :], db_col[:, b : b + 1])
         db_row = sb("db_row", [1, S], F32)
         nc.scalar.copy(db_row[:], row_ps[0:1, :, :].rearrange("p a b -> p (a b)"))
-        nc.scalar.dma_start(out_1, db_row[:])
+        nc.sync.dma_start(out_1, db_row[:])

@@ -25,7 +25,7 @@ BLOCKS = S // P
 PER_COLUMN = 16
 LINE = 4
 LOADED = P - 1
-BANKS = {"turned": 3, "product": 4}
+BANKS = {"factor0": 1, "factor1": 1, "factor2": 1, "factor3": 1, "work": 4}
 
 
 def tile_attend_gbias_wb_log_kernel(tc, xT, wT, ts, kb, us, y, wt, offs, out_0, out_1):
@@ -57,7 +57,7 @@ def tile_attend_gbias_wb_log_kernel(tc, xT, wT, ts, kb, us, y, wt, offs, out_0, 
 
         offsets = keep.tile([P, S // PER_COLUMN], U16, name="offsets")
         x_raw = sb("x_raw", [P, PACK, R], F32)
-        y_raw = sb("y_raw", [P, PACK, S], F32)
+        y_raw = [sb("y_raw%d" % half, [P, PACK, HALF], F32) for half in range(2)]
         w_raw = [sb("w_raw%d" % t, [P, T], F32) for t in range(PACK)]
         ts_table = sb("ts_table", [P, T], F32)
         kb_table = sb("kb_table", [P, T], F32)
@@ -73,15 +73,21 @@ def tile_attend_gbias_wb_log_kernel(tc, xT, wT, ts, kb, us, y, wt, offs, out_0, 
         w_planes = wT.rearrange("(p t) c -> t p c", t=PACK)
         for t in range(PACK):
             nc.sync.dma_start(w_raw[t][:], w_planes[t])
-        nc.sync.dma_start(y_raw[:], y.rearrange("(p t) s -> p t s", t=PACK))
+        y_planes = y.rearrange("(p t) s -> p t s", t=PACK)
+        for half in range(2):
+            nc.sync.dma_start(y_raw[half][:], y_planes[:, :, half * HALF : (half + 1) * HALF])
 
+        warm = sb("warm", [P, 1], F32)
+        nc.vector.memset(warm[:], 0.0)
+        warmed = sb("warmed", [P, 1], F32)
+        nc.scalar.activation(warmed[:], warm[:], ACT.Sigmoid)
         ident = sb("ident", [P, P], F32)
         make_identity(nc, ident[:])
 
         nc.vector.memset(ts_table[0:LOADED, :].bitcast(I32), 0)
-        nc.vector.memset(kb_table[0:LOADED, :].bitcast(I32), 0)
+        nc.gpsimd.memset(kb_table[0:LOADED, :].bitcast(I32), 0)
 
-        us_ps = bank("us_ps", "product")
+        us_ps = bank("us_ps", "work")
         for t in range(PACK):
             spread(us_ps[:, t, :], us_col[:, t : t + 1])
         us_row = sb("us_row", [P, PACK, P], F32)
@@ -93,7 +99,7 @@ def tile_attend_gbias_wb_log_kernel(tc, xT, wT, ts, kb, us, y, wt, offs, out_0, 
         for name, table in (("ts", ts_table), ("kb", kb_table)):
             picked = sb(name + "_picked", [P, S], F32)
             nc.vector.tensor_copy(picked[:], table[:].indirect(offsets[:]))
-            col_ps = bank(name + "_ps", "product")
+            col_ps = bank(name + "_ps", "work")
             for b in range(BLOCKS):
                 turn(col_ps[:, b, :], picked[:, b * P : (b + 1) * P])
             col = sb(name + "_col", [P, BLOCKS], F32)
@@ -103,8 +109,6 @@ def tile_attend_gbias_wb_log_kernel(tc, xT, wT, ts, kb, us, y, wt, offs, out_0, 
 
         window_0 = sb("window_0", [P, T], F32)
         nc.vector.memset(window_0[:].bitcast(I32), 0)
-        window_2 = sb("window_2", [P, T], F32)
-        nc.vector.memset(window_2[:].bitcast(I32), 0)
 
         x_d = sb("x_d", [P, R, PACK], BF16)
         weave(x_d[:], x_raw[:])
@@ -112,7 +116,7 @@ def tile_attend_gbias_wb_log_kernel(tc, xT, wT, ts, kb, us, y, wt, offs, out_0, 
         x_r = sb("x_r", [P, D, PACK], BF16)
         x_words = flat(x_d).bitcast(F32)
         for u in range(2):
-            xt_ps = bank("xt_ps", "turned")
+            xt_ps = bank("xt_ps", "factor%d" % (2 + u))
             for j in range(PACK):
                 turn(xt_ps[:, j, :], x_words[:, 2 * j + u : 2 * R : 2 * PACK])
             nc.scalar.copy(
@@ -120,14 +124,17 @@ def tile_attend_gbias_wb_log_kernel(tc, xT, wT, ts, kb, us, y, wt, offs, out_0, 
                 flat(xt_ps).bitcast(BF16).rearrange("m (j p e) -> m e p j", j=PACK, e=2),
             )
 
-        ts_row_ps = psum.tile([P, S], F32, name="ts_row_ps", tag="ts_row", bufs=1)
-        for b in range(BLOCKS):
-            spread(ts_row_ps[:, b * P : (b + 1) * P], ts_col[:, b : b + 1])
-        factor_planes = sb("factor_planes", [P, PACK, S], F32)
+        us_wt_ps = bank("us_wt_ps", "work")
         for t in range(PACK):
-            nc.scalar.activation(factor_planes[:, t, :], ts_row_ps[:], ACT.Copy, scale=us_wt_col[:, t : t + 1])
-        factor = sb("factor", [P, S, PACK], F32)
-        weave(factor[:], factor_planes[:])
+            spread(us_wt_ps[:, t, :], us_wt_col[:, t : t + 1])
+        factor_ps = []
+        for b in range(BLOCKS):
+            factor_t = sb("factor_t%d" % b, [P, PACK, P], F32)
+            nc.scalar.activation(factor_t[:], us_wt_ps[:], ACT.Copy, scale=ts_col[:, b : b + 1])
+            f_ps = bank("f_ps", "factor%d" % b)
+            for t in range(PACK):
+                turn(f_ps[:, t, :], factor_t[:, t, :])
+            factor_ps.append(f_ps)
 
         w_woven = [sb("w_woven%d" % half, [P, HALF, PACK], BF16) for half in range(2)]
         w_codes = [sb("w_codes%d" % half, [P, HALF], U32) for half in range(2)]
@@ -157,12 +164,16 @@ def tile_attend_gbias_wb_log_kernel(tc, xT, wT, ts, kb, us, y, wt, offs, out_0, 
         h_woven = [sb("h_woven%d" % half, [P, HALF, PACK], BF16) for half in range(2)]
         h_codes = sb("h_codes", [P, S], U32)
         h_scales = sb("h_scales", [P, S], U8)
+        nc.vector.memset(h_codes[:, HALF:].bitcast(I32), 0)
+        nc.vector.memset(h_scales[:, HALF:].bitcast(I32), 0)
+        window_1 = sb("window_1", [P, T], F32, tag="w_woven1")
+        nc.gpsimd.memset(window_1[:].bitcast(I32), 0)
         resid = sb("resid", [P, S, PACK], F32)
         y_woven = sb("y_woven", [P, S, PACK], F32)
         probs = []
         for b in range(BLOCKS):
             half, within = b // 2, slice((b % 2) * P, (b % 2 + 1) * P)
-            a_ps = bank("a_ps", "product")
+            a_ps = bank("a_ps", "work")
             nc.tensor.matmul_mx(
                 flat(a_ps),
                 lhsT=w_codes[half][:, within].bitcast(E4),
@@ -178,33 +189,13 @@ def tile_attend_gbias_wb_log_kernel(tc, xT, wT, ts, kb, us, y, wt, offs, out_0, 
             nc.scalar.activation(prob[:], scaled[:], ACT.Sigmoid, bias=kb_col[:, b : b + 1], scale=ts_col[:, b : b + 1])
             probs.append(prob)
             slots = slice(b * P, (b + 1) * P)
-            weave(y_woven[:, slots, :], y_raw[:, :, slots])
+            weave(y_woven[:, slots, :], y_raw[half][:, :, within])
+        window_2 = sb("window_2", [P, T], F32, tag="w_raw0")
+        nc.gpsimd.memset(window_2[:].bitcast(I32), 0)
 
-        for half in range(2):
-            blocks = (2 * half, 2 * half + 1)
-            for b in blocks:
-                slots = slice(b * P, (b + 1) * P)
-                p_ps = bank("p_ps", "turned")
-                for t in range(PACK):
-                    turn(p_ps[:, t, :], probs[b][:, t, :])
-                nc.vector.tensor_tensor(
-                    resid[:, slots, :], p_ps[:].rearrange("m t s -> m s t"), y_woven[:, slots, :], ALU.subtract
-                )
-            for b in blocks:
-                slots, within = slice(b * P, (b + 1) * P), slice((b % 2) * P, (b % 2 + 1) * P)
-                nc.vector.tensor_tensor(h_woven[half][:, within, :], resid[:, slots, :], factor[:, slots, :], ALU.mult)
-            slots = slice(half * HALF, (half + 1) * HALF)
-            nc.vector.quantize_mx(h_codes[:, slots].bitcast(E5), h_scales[:, slots], flat(h_woven[half]))
-
-        window_1 = sb("window_1", [P, T], F32, tag="h_woven1")
-        nc.vector.memset(window_1[:].bitcast(I32), 0)
-        windows = [window_0, window_1, window_2, window_0]
-
-        out_planes = out_0.rearrange("(p t) c -> t p c", t=PACK)
-        for t in range(PACK):
-            dw = sb("dw%d" % t, [P, S], F32)
+        def product(t, tag="work"):
             features = slice(t * P, (t + 1) * P)
-            o_ps = bank("o_ps", "product")
+            o_ps = bank("o_ps", tag)
             nc.tensor.matmul_mx(
                 flat(o_ps),
                 lhsT=xr_codes[:, features].bitcast(E4),
@@ -214,15 +205,45 @@ def tile_attend_gbias_wb_log_kernel(tc, xT, wT, ts, kb, us, y, wt, offs, out_0, 
                 start=True,
                 stop=True,
             )
-            nc.scalar.copy(dw[:], flat(o_ps))
-            nc.vector.tensor_copy(windows[t][:].indirect(offsets[:]), dw[:])
+            return flat(o_ps)
+
+        for half in range(2):
+            blocks = (2 * half, 2 * half + 1)
+            for b in blocks:
+                slots = slice(b * P, (b + 1) * P)
+                p_ps = bank("p_ps", "work")
+                for t in range(PACK):
+                    turn(p_ps[:, t, :], probs[b][:, t, :])
+                nc.vector.tensor_tensor(
+                    resid[:, slots, :], p_ps[:].rearrange("m t s -> m s t"), y_woven[:, slots, :], ALU.subtract
+                )
+            for b in blocks:
+                slots, within = slice(b * P, (b + 1) * P), slice((b % 2) * P, (b % 2 + 1) * P)
+                nc.vector.tensor_tensor(h_woven[half][:, within, :], factor_ps[b][:].rearrange("m t s -> m s t"), resid[:, slots, :], ALU.mult)
+            if half == 1:
+                early_ps = product(0, "factor2")
+            for b in blocks:
+                slots, within = slice(b * P, (b + 1) * P), slice((b % 2) * P * PACK, (b % 2 + 1) * P * PACK)
+                nc.vector.quantize_mx(h_codes[:, slots].bitcast(E5), h_scales[:, slots], flat(h_woven[half])[:, within])
+
+        windows = [window_0, window_1, window_2, window_1]
+        dw_early = sb("dw_early", [P, HALF], F32)
+        nc.scalar.copy(dw_early[:], early_ps[:, :HALF])
+        nc.vector.tensor_copy(window_0[:].indirect(offsets[:, : HALF // PER_COLUMN]), dw_early[:])
+
+        out_planes = out_0.rearrange("(p t) c -> t p c", t=PACK)
+        for t in (1, 0, 2, 3):
+            first = HALF if t == 0 else 0
+            dw = sb("dw%d" % t, [P, S - first], F32)
+            nc.scalar.copy(dw[:], product(t)[:, first:])
+            nc.vector.tensor_copy(windows[t][:].indirect(offsets[:, first // PER_COLUMN :]), dw[:])
             queue = nc.scalar if t == PACK - 1 else nc.sync
             queue.dma_start(out_planes[t], windows[t][:])
 
         g = sb("g", [P, PACK, S], F32, tag="w_raw2")
         for t in range(PACK):
             nc.scalar.activation(g[:, t, :], resid[:, :, t], ACT.Copy, scale=wt_col[:, t : t + 1])
-        sum_ps = bank("sum_ps", "product")
+        sum_ps = bank("sum_ps", "factor0")
         for b in range(BLOCKS):
             for t in range(PACK):
                 turn(sum_ps[:, b, :], g[:, t, b * P : (b + 1) * P], start=(t == 0), stop=(t == PACK - 1))
@@ -230,7 +251,7 @@ def tile_attend_gbias_wb_log_kernel(tc, xT, wT, ts, kb, us, y, wt, offs, out_0, 
         copied = sb("copied", [P, P], F32)
         for b in range(BLOCKS):
             nc.scalar.activation(copied[:], sum_ps[:, b, :], ACT.Copy, accum_out=db_col[:, b : b + 1])
-        row_ps = bank("row_ps", "product")
+        row_ps = bank("row_ps", "factor1")
         for b in range(BLOCKS):
             spread(row_ps[:, b, :], db_col[:, b : b + 1])
         db_row = sb("db_row", [1, S], F32)

@@ -49,12 +49,6 @@ def tile_attend_gbias_wb_log_kernel(tc, xT, wT, ts, kb, us, y, wt, offs, out_0, 
         def spread(out, column):
             turn(out, column.to_broadcast([P, P]))
 
-        def weave(woven, planes):
-            nc.scalar.copy(
-                woven.rearrange("p (c i) t -> p c t i", i=LINE),
-                planes.rearrange("p t (c i) -> p c t i", i=LINE),
-            )
-
         offsets = keep.tile([P, S // PER_COLUMN], U16, name="offsets")
         x_raw = sb("x_raw", [P, PACK, R], F32)
         y_raw = [sb("y_raw%d" % half, [P, PACK, HALF], F32) for half in range(2)]
@@ -64,8 +58,8 @@ def tile_attend_gbias_wb_log_kernel(tc, xT, wT, ts, kb, us, y, wt, offs, out_0, 
         us_col = sb("us_col", [P, PACK], F32)
         wt_col = sb("wt_col", [P, PACK], F32)
 
-        nc.sync.dma_start(x_raw[:], xT.rearrange("(p t) r -> p t r", t=PACK))
         nc.sync.dma_start(offsets[:], offs)
+        nc.sync.dma_start(x_raw[:], xT.rearrange("(p t) r -> p t r", t=PACK))
         nc.scalar.dma_start(ts_table[LOADED:P, :], ts[0:1, :])
         nc.scalar.dma_start(kb_table[LOADED:P, :], kb[0:1, :])
         nc.sync.dma_start(us_col[:], us.rearrange("(p t) o -> p (t o)", t=PACK))
@@ -85,7 +79,7 @@ def tile_attend_gbias_wb_log_kernel(tc, xT, wT, ts, kb, us, y, wt, offs, out_0, 
         make_identity(nc, ident[:])
 
         nc.vector.memset(ts_table[0:LOADED, :].bitcast(I32), 0)
-        nc.gpsimd.memset(kb_table[0:LOADED, :].bitcast(I32), 0)
+        nc.vector.memset(kb_table[0:LOADED, :].bitcast(I32), 0)
 
         us_ps = bank("us_ps", "work")
         for t in range(PACK):
@@ -111,14 +105,17 @@ def tile_attend_gbias_wb_log_kernel(tc, xT, wT, ts, kb, us, y, wt, offs, out_0, 
         nc.vector.memset(window_0[:].bitcast(I32), 0)
 
         x_d = sb("x_d", [P, R, PACK], BF16)
-        weave(x_d[:], x_raw[:])
+        nc.scalar.copy(
+            x_d[:].rearrange("p (j m) t -> p m t j", j=PACK),
+            x_raw[:].rearrange("p t (m j) -> p m t j", j=PACK),
+        )
 
         x_r = sb("x_r", [P, D, PACK], BF16)
         x_words = flat(x_d).bitcast(F32)
         for u in range(2):
             xt_ps = bank("xt_ps", "factor%d" % (2 + u))
             for j in range(PACK):
-                turn(xt_ps[:, j, :], x_words[:, 2 * j + u : 2 * R : 2 * PACK])
+                turn(xt_ps[:, j, :], x_words[:, 2 * j * P + u : 2 * (j + 1) * P : 2])
             nc.scalar.copy(
                 x_r[:, 2 * u * P : 2 * (u + 1) * P, :].rearrange("m (e p) j -> m e p j", e=2),
                 flat(xt_ps).bitcast(BF16).rearrange("m (j p e) -> m e p j", j=PACK, e=2),
@@ -136,13 +133,13 @@ def tile_attend_gbias_wb_log_kernel(tc, xT, wT, ts, kb, us, y, wt, offs, out_0, 
                 turn(f_ps[:, t, :], factor_t[:, t, :])
             factor_ps.append(f_ps)
 
-        w_woven = [sb("w_woven%d" % half, [P, HALF, PACK], BF16) for half in range(2)]
+        w_woven = sb("w_woven", [P, S, PACK], BF16)
         w_codes = [sb("w_codes%d" % half, [P, HALF], U32) for half in range(2)]
         w_scales = [sb("w_scales%d" % half, [P, HALF], U8) for half in range(2)]
 
-        def gather_w(t, half):
-            listed = offsets[:, half * HALF // PER_COLUMN : (half + 1) * HALF // PER_COLUMN]
-            nc.vector.tensor_copy(w_woven[half][:, :, t], w_raw[t][:].indirect(listed))
+        def gather_w(t, first, last):
+            listed = offsets[:, first // PER_COLUMN : last // PER_COLUMN]
+            nc.vector.tensor_copy(w_woven[:, first:last, t], w_raw[t][:].indirect(listed))
 
         def quantize_x(name, woven, tag):
             codes = sb(name + "_codes", [P, woven.shape[1]], U32, tag=tag)
@@ -150,26 +147,25 @@ def tile_attend_gbias_wb_log_kernel(tc, xT, wT, ts, kb, us, y, wt, offs, out_0, 
             nc.vector.quantize_mx(codes[:].bitcast(E4), scales[:], flat(woven))
             return codes, scales
 
-        gather_w(0, 0)
-        gather_w(0, 1)
+        gather_w(0, 0, S)
         xd_codes, xd_scales = quantize_x("xd", x_d, "w_raw0")
-        for t in (1, 2):
-            gather_w(t, 0)
-            gather_w(t, 1)
+        gather_w(1, 0, S)
+        gather_w(2, 0, S)
         xr_codes, xr_scales = quantize_x("xr", x_r, "w_raw2")
         for half in range(2):
-            gather_w(PACK - 1, half)
-            nc.vector.quantize_mx(w_codes[half][:].bitcast(E4), w_scales[half][:], flat(w_woven[half]))
+            gather_w(PACK - 1, half * HALF, (half + 1) * HALF)
+        for half in range(2):
+            columns = slice(half * HALF * PACK, (half + 1) * HALF * PACK)
+            nc.vector.quantize_mx(w_codes[half][:].bitcast(E4), w_scales[half][:], flat(w_woven)[:, columns])
 
         h_woven = [sb("h_woven%d" % half, [P, HALF, PACK], BF16) for half in range(2)]
         h_codes = sb("h_codes", [P, S], U32)
         h_scales = sb("h_scales", [P, S], U8)
         nc.vector.memset(h_codes[:, HALF:].bitcast(I32), 0)
         nc.vector.memset(h_scales[:, HALF:].bitcast(I32), 0)
-        window_1 = sb("window_1", [P, T], F32, tag="w_woven1")
+        window_1 = sb("window_1", [P, T], F32, tag="w_woven")
         nc.gpsimd.memset(window_1[:].bitcast(I32), 0)
-        resid = sb("resid", [P, S, PACK], F32)
-        y_woven = sb("y_woven", [P, S, PACK], F32)
+        resid = sb("resid", [P, PACK, S], F32)
         probs = []
         for b in range(BLOCKS):
             half, within = b // 2, slice((b % 2) * P, (b % 2 + 1) * P)
@@ -184,12 +180,10 @@ def tile_attend_gbias_wb_log_kernel(tc, xT, wT, ts, kb, us, y, wt, offs, out_0, 
                 stop=True,
             )
             scaled = sb("scaled%d" % b, [P, PACK, P], F32)
-            nc.vector.tensor_tensor(scaled[:], flat(a_ps).rearrange("p (m t) -> p t m", t=PACK), us_row[:], ALU.mult)
+            nc.vector.tensor_tensor(scaled[:], a_ps[:], us_row[:], ALU.mult)
             prob = sb("prob%d" % b, [P, PACK, P], F32)
             nc.scalar.activation(prob[:], scaled[:], ACT.Sigmoid, bias=kb_col[:, b : b + 1], scale=ts_col[:, b : b + 1])
             probs.append(prob)
-            slots = slice(b * P, (b + 1) * P)
-            weave(y_woven[:, slots, :], y_raw[half][:, :, within])
         window_2 = sb("window_2", [P, T], F32, tag="w_raw0")
         nc.gpsimd.memset(window_2[:].bitcast(I32), 0)
 
@@ -210,16 +204,19 @@ def tile_attend_gbias_wb_log_kernel(tc, xT, wT, ts, kb, us, y, wt, offs, out_0, 
         for half in range(2):
             blocks = (2 * half, 2 * half + 1)
             for b in blocks:
-                slots = slice(b * P, (b + 1) * P)
+                slots, within = slice(b * P, (b + 1) * P), slice((b % 2) * P, (b % 2 + 1) * P)
                 p_ps = bank("p_ps", "work")
                 for t in range(PACK):
                     turn(p_ps[:, t, :], probs[b][:, t, :])
-                nc.vector.tensor_tensor(
-                    resid[:, slots, :], p_ps[:].rearrange("m t s -> m s t"), y_woven[:, slots, :], ALU.subtract
-                )
+                nc.vector.tensor_tensor(resid[:, :, slots], p_ps[:], y_raw[half][:, :, within], ALU.subtract)
             for b in blocks:
                 slots, within = slice(b * P, (b + 1) * P), slice((b % 2) * P, (b % 2 + 1) * P)
-                nc.vector.tensor_tensor(h_woven[half][:, within, :], factor_ps[b][:].rearrange("m t s -> m s t"), resid[:, slots, :], ALU.mult)
+                nc.vector.tensor_tensor(
+                    h_woven[half][:, within, :].rearrange("m (c i) t -> m c t i", i=LINE),
+                    factor_ps[b][:].rearrange("m t (c i) -> m c t i", i=LINE),
+                    resid[:, :, slots].rearrange("m t (c i) -> m c t i", i=LINE),
+                    ALU.mult,
+                )
             if half == 1:
                 early_ps = product(0, "factor2")
             for b in blocks:
@@ -242,7 +239,7 @@ def tile_attend_gbias_wb_log_kernel(tc, xT, wT, ts, kb, us, y, wt, offs, out_0, 
 
         g = sb("g", [P, PACK, S], F32, tag="w_raw2")
         for t in range(PACK):
-            nc.scalar.activation(g[:, t, :], resid[:, :, t], ACT.Copy, scale=wt_col[:, t : t + 1])
+            nc.scalar.activation(g[:, t, :], resid[:, t, :], ACT.Copy, scale=wt_col[:, t : t + 1])
         sum_ps = bank("sum_ps", "factor0")
         for b in range(BLOCKS):
             for t in range(PACK):

@@ -101,8 +101,6 @@ def tile_attend_gbias_wb_log_kernel(tc, xT, wT, ts, kb, us, y, wt, offs, out_0, 
             listed_cols.append(col)
         ts_col, kb_col = listed_cols
 
-        window_0 = sb("window_0", [P, T], F32)
-        nc.vector.memset(window_0[:].bitcast(I32), 0)
 
         x_d = sb("x_d", [P, R, PACK], BF16)
         nc.scalar.copy(
@@ -163,8 +161,8 @@ def tile_attend_gbias_wb_log_kernel(tc, xT, wT, ts, kb, us, y, wt, offs, out_0, 
         h_scales = sb("h_scales", [P, S], U8)
         nc.vector.memset(h_codes[:, HALF:].bitcast(I32), 0)
         nc.vector.memset(h_scales[:, HALF:].bitcast(I32), 0)
-        window_1 = sb("window_1", [P, T], F32, tag="w_woven")
-        nc.gpsimd.memset(window_1[:].bitcast(I32), 0)
+        window_0 = sb("window_0", [P, T], F32, tag="w_woven")
+        nc.gpsimd.memset(window_0[:].bitcast(I32), 0)
         resid = sb("resid", [P, PACK, S], F32)
         probs = []
         for b in range(BLOCKS):
@@ -184,8 +182,8 @@ def tile_attend_gbias_wb_log_kernel(tc, xT, wT, ts, kb, us, y, wt, offs, out_0, 
             prob = sb("prob%d" % b, [P, PACK, P], F32)
             nc.scalar.activation(prob[:], scaled[:], ACT.Sigmoid, bias=kb_col[:, b : b + 1], scale=ts_col[:, b : b + 1])
             probs.append(prob)
-        window_2 = sb("window_2", [P, T], F32, tag="w_raw0")
-        nc.gpsimd.memset(window_2[:].bitcast(I32), 0)
+        window_1 = sb("window_1", [P, T], F32, tag="w_raw0")
+        nc.gpsimd.memset(window_1[:].bitcast(I32), 0)
 
         def product(t, tag="work"):
             features = slice(t * P, (t + 1) * P)
@@ -223,6 +221,8 @@ def tile_attend_gbias_wb_log_kernel(tc, xT, wT, ts, kb, us, y, wt, offs, out_0, 
                 slots, within = slice(b * P, (b + 1) * P), slice((b % 2) * P * PACK, (b % 2 + 1) * P * PACK)
                 nc.vector.quantize_mx(h_codes[:, slots].bitcast(E5), h_scales[:, slots], flat(h_woven[half])[:, within])
 
+        window_2 = sb("window_2", [P, T], F32, tag="h_woven0")
+        nc.gpsimd.memset(window_2[:].bitcast(I32), 0)
         windows = [window_0, window_1, window_2, window_1]
         dw_early = sb("dw_early", [P, HALF], F32)
         nc.scalar.copy(dw_early[:], early_ps[:, :HALF])
@@ -234,8 +234,7 @@ def tile_attend_gbias_wb_log_kernel(tc, xT, wT, ts, kb, us, y, wt, offs, out_0, 
             dw = sb("dw%d" % t, [P, S - first], F32)
             nc.scalar.copy(dw[:], product(t)[:, first:])
             nc.vector.tensor_copy(windows[t][:].indirect(offsets[:, first // PER_COLUMN :]), dw[:])
-            queue = nc.scalar if t == PACK - 1 else nc.sync
-            queue.dma_start(out_planes[t], windows[t][:])
+            nc.sync.dma_start(out_planes[t], windows[t][:])
 
         g = sb("g", [P, PACK, S], F32, tag="w_raw2")
         for t in range(PACK):
@@ -253,4 +252,4 @@ def tile_attend_gbias_wb_log_kernel(tc, xT, wT, ts, kb, us, y, wt, offs, out_0, 
             spread(row_ps[:, b, :], db_col[:, b : b + 1])
         db_row = sb("db_row", [1, S], F32)
         nc.scalar.copy(db_row[:], row_ps[0:1, :, :].rearrange("p a b -> p (a b)"))
-        nc.sync.dma_start(out_1, db_row[:])
+        nc.scalar.dma_start(out_1, db_row[:])

@@ -58,12 +58,12 @@ def tile_attend_gbias_wb_log_kernel(tc, xT, wT, ts, kb, us, y, wt, offs, out_0, 
         us_col = sb("us_col", [P, PACK], F32)
         wt_col = sb("wt_col", [P, PACK], F32)
 
-        nc.sync.dma_start(offsets[:], offs)
         nc.sync.dma_start(x_raw[:], xT.rearrange("(p t) r -> p t r", t=PACK))
+        nc.sync.dma_start(offsets[:], offs)
         nc.scalar.dma_start(ts_table[LOADED:P, :], ts[0:1, :])
         nc.scalar.dma_start(kb_table[LOADED:P, :], kb[0:1, :])
-        nc.sync.dma_start(us_col[:], us.rearrange("(p t) o -> p (t o)", t=PACK))
-        nc.sync.dma_start(wt_col[:], wt.rearrange("(p t) o -> p (t o)", t=PACK))
+        nc.scalar.dma_start(us_col[:], us.rearrange("(p t) o -> p (t o)", t=PACK))
+        nc.scalar.dma_start(wt_col[:], wt.rearrange("(p t) o -> p (t o)", t=PACK))
         w_planes = wT.rearrange("(p t) c -> t p c", t=PACK)
         for t in range(PACK):
             nc.sync.dma_start(w_raw[t][:], w_planes[t])
@@ -148,19 +148,20 @@ def tile_attend_gbias_wb_log_kernel(tc, xT, wT, ts, kb, us, y, wt, offs, out_0, 
         gather_w(0, 0, S)
         xd_codes, xd_scales = quantize_x("xd", x_d, "w_raw0")
         gather_w(1, 0, S)
+        xr_codes, xr_scales = quantize_x("xr", x_r, "w_raw1")
         gather_w(2, 0, S)
-        xr_codes, xr_scales = quantize_x("xr", x_r, "w_raw2")
         for half in range(2):
             gather_w(PACK - 1, half * HALF, (half + 1) * HALF)
-        for half in range(2):
-            columns = slice(half * HALF * PACK, (half + 1) * HALF * PACK)
-            nc.vector.quantize_mx(w_codes[half][:].bitcast(E4), w_scales[half][:], flat(w_woven)[:, columns])
+            for b in range(2):
+                within = slice(b * P, (b + 1) * P)
+                columns = slice((2 * half + b) * P * PACK, (2 * half + b + 1) * P * PACK)
+                nc.vector.quantize_mx(w_codes[half][:, within].bitcast(E4), w_scales[half][:, within], flat(w_woven)[:, columns])
 
         h_woven = [sb("h_woven%d" % half, [P, HALF, PACK], BF16) for half in range(2)]
-        h_codes = sb("h_codes", [P, S], U32)
-        h_scales = sb("h_scales", [P, S], U8)
-        nc.vector.memset(h_codes[:, HALF:].bitcast(I32), 0)
-        nc.vector.memset(h_scales[:, HALF:].bitcast(I32), 0)
+        h_codes = sb("h_codes", [P, HALF + S], U32)
+        h_scales = sb("h_scales", [P, HALF + S], U8)
+        nc.vector.memset(h_codes[:, :HALF].bitcast(I32), 0)
+        nc.vector.memset(h_scales[:, :HALF].bitcast(I32), 0)
         window_0 = sb("window_0", [P, T], F32, tag="w_woven")
         nc.gpsimd.memset(window_0[:].bitcast(I32), 0)
         resid = sb("resid", [P, PACK, S], F32)
@@ -185,15 +186,15 @@ def tile_attend_gbias_wb_log_kernel(tc, xT, wT, ts, kb, us, y, wt, offs, out_0, 
         window_1 = sb("window_1", [P, T], F32, tag="w_raw0")
         nc.gpsimd.memset(window_1[:].bitcast(I32), 0)
 
-        def product(t, tag="work"):
+        def product(t, first, tag="work"):
             features = slice(t * P, (t + 1) * P)
             o_ps = bank("o_ps", tag)
             nc.tensor.matmul_mx(
                 flat(o_ps),
                 lhsT=xr_codes[:, features].bitcast(E4),
                 lhsT_scale=xr_scales[:, features],
-                rhs=h_codes[:].bitcast(E5),
-                rhs_scale=h_scales[:],
+                rhs=h_codes[:, first : first + S].bitcast(E5),
+                rhs_scale=h_scales[:, first : first + S],
                 start=True,
                 stop=True,
             )
@@ -215,28 +216,27 @@ def tile_attend_gbias_wb_log_kernel(tc, xT, wT, ts, kb, us, y, wt, offs, out_0, 
                     resid[:, :, slots].rearrange("m t (c i) -> m c t i", i=LINE),
                     ALU.mult,
                 )
-            if half == 1:
-                early_ps = product(0, "factor2")
             for b in blocks:
-                slots, within = slice(b * P, (b + 1) * P), slice((b % 2) * P * PACK, (b % 2 + 1) * P * PACK)
+                slots, within = slice(HALF + b * P, HALF + (b + 1) * P), slice((b % 2) * P * PACK, (b % 2 + 1) * P * PACK)
                 nc.vector.quantize_mx(h_codes[:, slots].bitcast(E5), h_scales[:, slots], flat(h_woven[half])[:, within])
 
         window_2 = sb("window_2", [P, T], F32, tag="h_woven0")
         nc.gpsimd.memset(window_2[:].bitcast(I32), 0)
-        windows = [window_0, window_1, window_2, window_1]
-        dw_early = sb("dw_early", [P, HALF], F32)
-        nc.scalar.copy(dw_early[:], early_ps[:, :HALF])
-        nc.vector.tensor_copy(window_0[:].indirect(offsets[:, : HALF // PER_COLUMN]), dw_early[:])
+        windows = [window_0, window_1, window_2, window_0]
+        for t, tag in ((0, "factor0"), (1, "factor2")):
+            dw_early = sb("dw_early%d" % t, [P, HALF], F32)
+            nc.scalar.copy(dw_early[:], product(t, 0, tag)[:, HALF:])
+            nc.vector.tensor_copy(windows[t][:].indirect(offsets[:, : HALF // PER_COLUMN]), dw_early[:])
 
         out_planes = out_0.rearrange("(p t) c -> t p c", t=PACK)
-        for t in (1, 0, 2, 3):
-            first = HALF if t == 0 else 0
+        for t in range(PACK):
+            first = HALF if t < 2 else 0
             dw = sb("dw%d" % t, [P, S - first], F32)
-            nc.scalar.copy(dw[:], product(t)[:, first:])
+            nc.scalar.copy(dw[:], product(t, HALF)[:, first:])
             nc.vector.tensor_copy(windows[t][:].indirect(offsets[:, first // PER_COLUMN :]), dw[:])
             nc.sync.dma_start(out_planes[t], windows[t][:])
 
-        g = sb("g", [P, PACK, S], F32, tag="w_raw2")
+        g = sb("g", [P, PACK, S], F32, tag="w_raw1")
         for t in range(PACK):
             nc.scalar.activation(g[:, t, :], resid[:, t, :], ACT.Copy, scale=wt_col[:, t : t + 1])
         sum_ps = bank("sum_ps", "factor0")

@@ -71,10 +71,6 @@ def tile_attend_gbias_wb_log_kernel(tc, xT, wT, ts, kb, us, y, wt, offs, out_0, 
         for half in range(2):
             nc.sync.dma_start(y_raw[half][:], y_planes[:, :, half * HALF : (half + 1) * HALF])
 
-        warm = sb("warm", [P, 1], F32)
-        nc.vector.memset(warm[:], 0.0)
-        warmed = sb("warmed", [P, 1], F32)
-        nc.scalar.activation(warmed[:], warm[:], ACT.Sigmoid)
         ident = sb("ident", [P, P], F32)
         make_identity(nc, ident[:])
 

@@ -24,6 +24,7 @@ HALF = S // 2
 BLOCKS = S // P
 PER_COLUMN = 16
 LINE = 4
+PAIR = 2
 LOADED = P - 1
 BANKS = {"factor0": 1, "factor1": 1, "factor2": 1, "factor3": 1, "work": 4}
 
@@ -153,14 +154,14 @@ def tile_attend_gbias_wb_log_kernel(tc, xT, wT, ts, kb, us, y, wt, offs, out_0, 
                 columns = slice((2 * half + b) * P * PACK, (2 * half + b + 1) * P * PACK)
                 nc.vector.quantize_mx(w_codes[half][:, within].bitcast(E4), w_scales[half][:, within], flat(w_woven)[:, columns])
 
-        h_woven = [sb("h_woven%d" % half, [P, HALF, PACK], BF16) for half in range(2)]
+        h_first = [sb("h_first%d" % b, [P, P, PACK], BF16) for b in range(2)]
         h_codes = sb("h_codes", [P, HALF + S], U32)
         h_scales = sb("h_scales", [P, HALF + S], U8)
         nc.vector.memset(h_codes[:, :HALF].bitcast(I32), 0)
         nc.vector.memset(h_scales[:, :HALF].bitcast(I32), 0)
         window_0 = sb("window_0", [P, T], F32, tag="w_woven")
         nc.gpsimd.memset(window_0[:].bitcast(I32), 0)
-        resid = sb("resid", [P, PACK, S], F32)
+        resid = sb("resid", [P, PACK, HALF], F32)
         probs = []
         for b in range(BLOCKS):
             half, within = b // 2, slice((b % 2) * P, (b % 2 + 1) * P)
@@ -179,6 +180,8 @@ def tile_attend_gbias_wb_log_kernel(tc, xT, wT, ts, kb, us, y, wt, offs, out_0, 
             prob = sb("prob%d" % b, [P, PACK, P], F32)
             nc.scalar.activation(prob[:], scaled[:], ACT.Sigmoid, bias=kb_col[:, b : b + 1], scale=ts_col[:, b : b + 1])
             probs.append(prob)
+        woven_factor = sb("woven_factor", [P, P, PACK], F32, tag="scaled3")
+        nc.scalar.copy(woven_factor[:], factor_ps[2][:].rearrange("m t i -> m i t"))
         window_1 = sb("window_1", [P, T], F32, tag="w_raw0")
         nc.gpsimd.memset(window_1[:].bitcast(I32), 0)
 
@@ -198,29 +201,47 @@ def tile_attend_gbias_wb_log_kernel(tc, xT, wT, ts, kb, us, y, wt, offs, out_0, 
 
         for half in range(2):
             blocks = (2 * half, 2 * half + 1)
+            if half:
+                h_second = sb("h_second", [P, HALF, PACK], BF16)
+                last_resid = sb("last_resid", [P, PACK, P], F32, tag="h_first0")
+                woven_resid = sb("woven_resid", [P, P, PACK], F32, tag="h_first1")
             for b in blocks:
                 slots, within = slice(b * P, (b + 1) * P), slice((b % 2) * P, (b % 2 + 1) * P)
                 p_ps = bank("p_ps", "work")
                 for t in range(PACK):
                     turn(p_ps[:, t, :], probs[b][:, t, :])
-                nc.vector.tensor_tensor(resid[:, :, slots], p_ps[:], y_raw[half][:, :, within], ALU.subtract)
+                if b == 2:
+                    nc.vector.tensor_tensor(
+                        woven_resid[:].rearrange("m (c i) t -> m c t i", i=PAIR),
+                        p_ps[:].rearrange("m t (c i) -> m c t i", i=PAIR),
+                        y_raw[half][:, :, within].rearrange("m t (c i) -> m c t i", i=PAIR),
+                        ALU.subtract,
+                    )
+                else:
+                    nc.vector.tensor_tensor(last_resid[:] if half else resid[:, :, slots], p_ps[:], y_raw[half][:, :, within], ALU.subtract)
             for b in blocks:
                 slots, within = slice(b * P, (b + 1) * P), slice((b % 2) * P, (b % 2 + 1) * P)
+                if b == 2:
+                    nc.gpsimd.tensor_tensor(h_second[:, within, :], woven_factor[:], woven_resid[:], ALU.mult)
+                    continue
                 nc.vector.tensor_tensor(
-                    h_woven[half][:, within, :].rearrange("m (c i) t -> m c t i", i=LINE),
+                    (h_second[:, within, :] if half else h_first[b][:]).rearrange("m (c i) t -> m c t i", i=LINE),
                     factor_ps[b][:].rearrange("m t (c i) -> m c t i", i=LINE),
-                    resid[:, :, slots].rearrange("m t (c i) -> m c t i", i=LINE),
+                    (last_resid[:] if half else resid[:, :, slots]).rearrange("m t (c i) -> m c t i", i=LINE),
                     ALU.mult,
                 )
+            if half:
+                nc.vector.quantize_mx(h_codes[:, S:].bitcast(E5), h_scales[:, S:], flat(h_second))
+                continue
             for b in blocks:
                 slots, within = slice(HALF + b * P, HALF + (b + 1) * P), slice((b % 2) * P * PACK, (b % 2 + 1) * P * PACK)
-                nc.vector.quantize_mx(h_codes[:, slots].bitcast(E5), h_scales[:, slots], flat(h_woven[half])[:, within])
+                nc.vector.quantize_mx(h_codes[:, slots].bitcast(E5), h_scales[:, slots], flat(h_first[b]))
 
-        window_2 = sb("window_2", [P, T], F32, tag="h_woven0")
+        window_2 = sb("window_2", [P, T], F32, tag="h_second")
         nc.gpsimd.memset(window_2[:].bitcast(I32), 0)
         windows = [window_0, window_1, window_2, window_0]
-        for t, tag in ((0, "factor0"), (1, "factor2")):
-            dw_early = sb("dw_early%d" % t, [P, HALF], F32)
+        for t, tag in ((0, "factor0"), (1, "factor3")):
+            dw_early = sb("dw_early%d" % t, [P, HALF], F32, tag="scaled3" if t else None)
             nc.scalar.copy(dw_early[:], product(t, 0, tag)[:, HALF:])
             nc.vector.tensor_copy(windows[t][:].indirect(offsets[:, : HALF // PER_COLUMN]), dw_early[:])
 
@@ -234,7 +255,10 @@ def tile_attend_gbias_wb_log_kernel(tc, xT, wT, ts, kb, us, y, wt, offs, out_0, 
 
         g = sb("g", [P, PACK, S], F32, tag="w_raw1")
         for t in range(PACK):
-            nc.scalar.activation(g[:, t, :], resid[:, t, :], ACT.Copy, scale=wt_col[:, t : t + 1])
+            scale = wt_col[:, t : t + 1]
+            nc.scalar.activation(g[:, t, :HALF], resid[:, t, :], ACT.Copy, scale=scale)
+            nc.scalar.activation(g[:, t, HALF : HALF + P], woven_resid[:, :, t], ACT.Copy, scale=scale)
+            nc.scalar.activation(g[:, t, HALF + P :], last_resid[:, t, :], ACT.Copy, scale=scale)
         sum_ps = bank("sum_ps", "factor0")
         for b in range(BLOCKS):
             for t in range(PACK):

@@ -33,6 +33,7 @@ def tile_attend_gbias_wb_log_kernel(tc, xT, wT, ts, kb, us, y, wt, offs, out_0, 
     nc = tc.nc
     with ExitStack() as ctx:
         keep = ctx.enter_context(tc.tile_pool(name="keep", bufs=1))
+        late = ctx.enter_context(tc.tile_pool(name="late", bufs=1))
         psum = ctx.enter_context(tc.psum_pool(name="psum", bufs=4))
 
         def sb(name, shape, dtype, tag=None):
@@ -155,10 +156,8 @@ def tile_attend_gbias_wb_log_kernel(tc, xT, wT, ts, kb, us, y, wt, offs, out_0, 
                 nc.vector.quantize_mx(w_codes[half][:, within].bitcast(E4), w_scales[half][:, within], flat(w_woven)[:, columns])
 
         h_first = [sb("h_first%d" % b, [P, P, PACK], BF16) for b in range(2)]
-        h_codes = sb("h_codes", [P, HALF + S], U32)
-        h_scales = sb("h_scales", [P, HALF + S], U8)
-        nc.vector.memset(h_codes[:, :HALF].bitcast(I32), 0)
-        nc.vector.memset(h_scales[:, :HALF].bitcast(I32), 0)
+        h_codes = [sb("h_codes%d" % half, [P, HALF], U32) for half in range(2)]
+        h_scales = [sb("h_scales%d" % half, [P, HALF], U8) for half in range(2)]
         window_0 = sb("window_0", [P, T], F32, tag="w_woven")
         nc.gpsimd.memset(window_0[:].bitcast(I32), 0)
         resid = sb("resid", [P, PACK, HALF], F32)
@@ -185,24 +184,22 @@ def tile_attend_gbias_wb_log_kernel(tc, xT, wT, ts, kb, us, y, wt, offs, out_0, 
         window_1 = sb("window_1", [P, T], F32, tag="w_raw0")
         nc.gpsimd.memset(window_1[:].bitcast(I32), 0)
 
-        def product(t, first, tag="work"):
+        def product(t, half, out):
             features = slice(t * P, (t + 1) * P)
-            o_ps = bank("o_ps", tag)
             nc.tensor.matmul_mx(
-                flat(o_ps),
+                out,
                 lhsT=xr_codes[:, features].bitcast(E4),
                 lhsT_scale=xr_scales[:, features],
-                rhs=h_codes[:, first : first + S].bitcast(E5),
-                rhs_scale=h_scales[:, first : first + S],
+                rhs=h_codes[half][:].bitcast(E5),
+                rhs_scale=h_scales[half][:],
                 start=True,
                 stop=True,
             )
-            return flat(o_ps)
 
         for half in range(2):
             blocks = (2 * half, 2 * half + 1)
             if half:
-                h_second = sb("h_second", [P, HALF, PACK], BF16)
+                h_second = late.tile([P, HALF, PACK], BF16, name="h_second", offset=4 * T - 2 * P * PACK, align_bytes=64)
                 last_resid = sb("last_resid", [P, PACK, P], F32, tag="h_first0")
                 woven_resid = sb("woven_resid", [P, P, PACK], F32, tag="h_first1")
             for b in blocks:
@@ -231,45 +228,53 @@ def tile_attend_gbias_wb_log_kernel(tc, xT, wT, ts, kb, us, y, wt, offs, out_0, 
                     ALU.mult,
                 )
             if half:
-                nc.vector.quantize_mx(h_codes[:, S:].bitcast(E5), h_scales[:, S:], flat(h_second))
+                nc.vector.quantize_mx(h_codes[1][:].bitcast(E5), h_scales[1][:], flat(h_second))
                 continue
             for b in blocks:
-                slots, within = slice(HALF + b * P, HALF + (b + 1) * P), slice((b % 2) * P * PACK, (b % 2 + 1) * P * PACK)
-                nc.vector.quantize_mx(h_codes[:, slots].bitcast(E5), h_scales[:, slots], flat(h_first[b]))
+                slots = slice(b * P, (b + 1) * P)
+                nc.vector.quantize_mx(h_codes[0][:, slots].bitcast(E5), h_scales[0][:, slots], flat(h_first[b]))
 
-        window_2 = sb("window_2", [P, T], F32, tag="h_second")
+        window_2 = late.tile([P, T], F32, name="window_2", offset=0, align_bytes=64)
         nc.gpsimd.memset(window_2[:].bitcast(I32), 0)
-        windows = [window_0, window_1, window_2, window_0]
-        for t, tag in ((0, "factor0"), (1, "factor3")):
-            dw_early = sb("dw_early%d" % t, [P, HALF], F32, tag="scaled3" if t else None)
-            nc.scalar.copy(dw_early[:], product(t, 0, tag)[:, HALF:])
-            nc.vector.tensor_copy(windows[t][:].indirect(offsets[:, : HALF // PER_COLUMN]), dw_early[:])
+        window_3 = late.tile([P, T], F32, name="window_3", offset=4 * T, align_bytes=64)
+        nc.gpsimd.memset(window_3[:].bitcast(I32), 0)
+        windows = [window_0, window_1, window_2, window_3]
 
         out_planes = out_0.rearrange("(p t) c -> t p c", t=PACK)
         for t in range(PACK):
-            first = HALF if t < 2 else 0
-            dw = sb("dw%d" % t, [P, S - first], F32)
-            nc.scalar.copy(dw[:], product(t, HALF)[:, first:])
-            nc.vector.tensor_copy(windows[t][:].indirect(offsets[:, first // PER_COLUMN :]), dw[:])
+            o_ps = bank("o_ps", "factor%d" % t)
+            product(t, 0, flat(o_ps)[:, :HALF])
+            dw = sb("dw_first%d" % t, [P, HALF], F32)
+            nc.scalar.copy(dw[:], flat(o_ps)[:, :HALF])
+            nc.scalar.activation(windows[t][:].indirect(offsets[:, : HALF // PER_COLUMN]), dw[:], ACT.Copy)
+        for t in range(PACK):
+            o_ps = bank("o_ps", "work")
+            product(t, 1, flat(o_ps)[:, :HALF])
+            dw = sb("dw_second%d" % t, [P, HALF], F32, tag="dw_second%d" % (t % 2))
+            nc.vector.tensor_copy(dw[:], flat(o_ps)[:, :HALF])
+            nc.vector.tensor_copy(windows[t][:].indirect(offsets[:, HALF // PER_COLUMN :]), dw[:])
             nc.sync.dma_start(out_planes[t], windows[t][:])
 
-        g = sb("g", [P, PACK, S], F32, tag="w_raw1")
+        g_first = sb("g_first", [P, PACK, HALF], F32)
+        g_second = sb("g_second", [P, PACK, HALF], F32, tag="dw_first3")
+        for t in range(PACK):
+            nc.scalar.activation(g_first[:, t, :], resid[:, t, :], ACT.Copy, scale=wt_col[:, t : t + 1])
         for t in range(PACK):
             scale = wt_col[:, t : t + 1]
-            nc.scalar.activation(g[:, t, :HALF], resid[:, t, :], ACT.Copy, scale=scale)
-            nc.scalar.activation(g[:, t, HALF : HALF + P], woven_resid[:, :, t], ACT.Copy, scale=scale)
-            nc.scalar.activation(g[:, t, HALF + P :], last_resid[:, t, :], ACT.Copy, scale=scale)
-        sum_ps = bank("sum_ps", "factor0")
+            nc.scalar.activation(g_second[:, t, :P], woven_resid[:, :, t], ACT.Copy, scale=scale)
+            nc.scalar.activation(g_second[:, t, P:], last_resid[:, t, :], ACT.Copy, scale=scale)
+        sum_ps = bank("sum_ps", "factor3")
         for b in range(BLOCKS):
+            g = g_second if b // 2 else g_first
             for t in range(PACK):
-                turn(sum_ps[:, b, :], g[:, t, b * P : (b + 1) * P], start=(t == 0), stop=(t == PACK - 1))
-        db_col = sb("db_col", [P, BLOCKS], F32)
+                turn(sum_ps[:, b, :], g[:, t, (b % 2) * P : (b % 2 + 1) * P], start=(t == 0), stop=(t == PACK - 1))
+        db_col = sb("db_col", [P, P], F32)
+        nc.vector.memset(db_col[:], 0.0)
         copied = sb("copied", [P, P], F32)
         for b in range(BLOCKS):
             nc.scalar.activation(copied[:], sum_ps[:, b, :], ACT.Copy, accum_out=db_col[:, b : b + 1])
         row_ps = bank("row_ps", "factor1")
-        for b in range(BLOCKS):
-            spread(row_ps[:, b, :], db_col[:, b : b + 1])
-        db_row = sb("db_row", [1, S], F32)
-        nc.scalar.copy(db_row[:], row_ps[0:1, :, :].rearrange("p a b -> p (a b)"))
-        nc.scalar.dma_start(out_1, db_row[:])
+        turn(row_ps[:, 0, :], db_col[:])
+        db_rows = sb("db_rows", [BLOCKS, P], F32)
+        nc.scalar.copy(db_rows[:], row_ps[0:BLOCKS, 0, :])
+        nc.scalar.dma_start(out_1.rearrange("o (b n) -> (o b) n", b=BLOCKS), db_rows[:])

@@ -33,7 +33,6 @@ def tile_attend_gbias_wb_log_kernel(tc, xT, wT, ts, kb, us, y, wt, offs, out_0, 
     nc = tc.nc
     with ExitStack() as ctx:
         keep = ctx.enter_context(tc.tile_pool(name="keep", bufs=1))
-        late = ctx.enter_context(tc.tile_pool(name="late", bufs=1))
         psum = ctx.enter_context(tc.psum_pool(name="psum", bufs=4))
 
         def sb(name, shape, dtype, tag=None):
@@ -98,6 +97,10 @@ def tile_attend_gbias_wb_log_kernel(tc, xT, wT, ts, kb, us, y, wt, offs, out_0, 
             nc.scalar.copy(col[:], col_ps[:, :, LOADED])
             listed_cols.append(col)
         ts_col, kb_col = listed_cols
+        window_2 = sb("window_2", [P, T], F32, tag="ts_table")
+        nc.gpsimd.memset(window_2[:].bitcast(I32), 0)
+        window_3 = sb("window_3", [P, T], F32, tag="kb_table")
+        nc.gpsimd.memset(window_3[:].bitcast(I32), 0)
 
 
         x_d = sb("x_d", [P, R, PACK], BF16)
@@ -199,7 +202,7 @@ def tile_attend_gbias_wb_log_kernel(tc, xT, wT, ts, kb, us, y, wt, offs, out_0, 
         for half in range(2):
             blocks = (2 * half, 2 * half + 1)
             if half:
-                h_second = late.tile([P, HALF, PACK], BF16, name="h_second", offset=4 * T - 2 * P * PACK, align_bytes=64)
+                h_second = sb("h_second", [P, HALF, PACK], BF16)
                 last_resid = sb("last_resid", [P, PACK, P], F32, tag="h_first0")
                 woven_resid = sb("woven_resid", [P, P, PACK], F32, tag="h_first1")
             for b in blocks:
@@ -234,10 +237,6 @@ def tile_attend_gbias_wb_log_kernel(tc, xT, wT, ts, kb, us, y, wt, offs, out_0, 
                 slots = slice(b * P, (b + 1) * P)
                 nc.vector.quantize_mx(h_codes[0][:, slots].bitcast(E5), h_scales[0][:, slots], flat(h_first[b]))
 
-        window_2 = late.tile([P, T], F32, name="window_2", offset=0, align_bytes=64)
-        nc.gpsimd.memset(window_2[:].bitcast(I32), 0)
-        window_3 = late.tile([P, T], F32, name="window_3", offset=4 * T, align_bytes=64)
-        nc.gpsimd.memset(window_3[:].bitcast(I32), 0)
         windows = [window_0, window_1, window_2, window_3]
 
         out_planes = out_0.rearrange("(p t) c -> t p c", t=PACK)
@@ -256,13 +255,13 @@ def tile_attend_gbias_wb_log_kernel(tc, xT, wT, ts, kb, us, y, wt, offs, out_0, 
             nc.sync.dma_start(out_planes[t], windows[t][:])
 
         g_first = sb("g_first", [P, PACK, HALF], F32)
-        g_second = sb("g_second", [P, PACK, HALF], F32, tag="dw_first3")
+        g_second = sb("g_second", [P, PACK, HALF], F32, tag="h_second")
         for t in range(PACK):
             nc.scalar.activation(g_first[:, t, :], resid[:, t, :], ACT.Copy, scale=wt_col[:, t : t + 1])
         for t in range(PACK):
             scale = wt_col[:, t : t + 1]
-            nc.scalar.activation(g_second[:, t, :P], woven_resid[:, :, t], ACT.Copy, scale=scale)
-            nc.scalar.activation(g_second[:, t, P:], last_resid[:, t, :], ACT.Copy, scale=scale)
+            nc.gpsimd.tensor_scalar(g_second[:, t, :P], woven_resid[:, :, t], scale, 0.0, ALU.mult, ALU.add)
+            nc.gpsimd.tensor_scalar(g_second[:, t, P:], last_resid[:, t, :], scale, 0.0, ALU.mult, ALU.add)
         sum_ps = bank("sum_ps", "factor3")
         for b in range(BLOCKS):
             g = g_second if b // 2 else g_first
@@ -270,7 +269,7 @@ def tile_attend_gbias_wb_log_kernel(tc, xT, wT, ts, kb, us, y, wt, offs, out_0, 
                 turn(sum_ps[:, b, :], g[:, t, (b % 2) * P : (b % 2 + 1) * P], start=(t == 0), stop=(t == PACK - 1))
         db_col = sb("db_col", [P, P], F32)
         nc.vector.memset(db_col[:], 0.0)
-        copied = sb("copied", [P, P], F32)
+        copied = sb("copied", [P, P], F32, tag="dw_first3")
         for b in range(BLOCKS):
             nc.scalar.activation(copied[:], sum_ps[:, b, :], ACT.Copy, accum_out=db_col[:, b : b + 1])
         row_ps = bank("row_ps", "factor1")

@@ -25,6 +25,7 @@ BLOCKS = S // P
 PER_COLUMN = 16
 LINE = 4
 PAIR = 2
+LATE = 4 * T - 2 * P * PACK
 LOADED = P - 1
 BANKS = {"factor0": 1, "factor1": 1, "factor2": 1, "factor3": 1, "work": 4}
 
@@ -33,6 +34,7 @@ def tile_attend_gbias_wb_log_kernel(tc, xT, wT, ts, kb, us, y, wt, offs, out_0, 
     nc = tc.nc
     with ExitStack() as ctx:
         keep = ctx.enter_context(tc.tile_pool(name="keep", bufs=1))
+        late = ctx.enter_context(tc.tile_pool(name="late", bufs=1))
         psum = ctx.enter_context(tc.psum_pool(name="psum", bufs=4))
 
         def sb(name, shape, dtype, tag=None):
@@ -97,10 +99,10 @@ def tile_attend_gbias_wb_log_kernel(tc, xT, wT, ts, kb, us, y, wt, offs, out_0, 
             nc.scalar.copy(col[:], col_ps[:, :, LOADED])
             listed_cols.append(col)
         ts_col, kb_col = listed_cols
-        window_2 = sb("window_2", [P, T], F32, tag="ts_table")
+        window_1 = sb("window_1", [P, T], F32, tag="ts_table")
+        nc.gpsimd.memset(window_1[:].bitcast(I32), 0)
+        window_2 = sb("window_2", [P, T], F32, tag="kb_table")
         nc.gpsimd.memset(window_2[:].bitcast(I32), 0)
-        window_3 = sb("window_3", [P, T], F32, tag="kb_table")
-        nc.gpsimd.memset(window_3[:].bitcast(I32), 0)
 
 
         x_d = sb("x_d", [P, R, PACK], BF16)
@@ -131,6 +133,9 @@ def tile_attend_gbias_wb_log_kernel(tc, xT, wT, ts, kb, us, y, wt, offs, out_0, 
             for t in range(PACK):
                 turn(f_ps[:, t, :], factor_t[:, t, :])
             factor_ps.append(f_ps)
+        woven_factor = sb("woven_factor", [P, HALF, PACK], F32)
+        for b in range(2):
+            nc.scalar.copy(woven_factor[:, b * P : (b + 1) * P, :], factor_ps[2 * b][:].rearrange("m t i -> m i t"))
 
         w_woven = sb("w_woven", [P, S, PACK], BF16)
         w_codes = [sb("w_codes%d" % half, [P, HALF], U32) for half in range(2)]
@@ -158,12 +163,11 @@ def tile_attend_gbias_wb_log_kernel(tc, xT, wT, ts, kb, us, y, wt, offs, out_0, 
                 columns = slice((2 * half + b) * P * PACK, (2 * half + b + 1) * P * PACK)
                 nc.vector.quantize_mx(w_codes[half][:, within].bitcast(E4), w_scales[half][:, within], flat(w_woven)[:, columns])
 
-        h_first = [sb("h_first%d" % b, [P, P, PACK], BF16) for b in range(2)]
-        h_codes = [sb("h_codes%d" % half, [P, HALF], U32) for half in range(2)]
+        h_first = late.tile([P, HALF, PACK], BF16, name="h_first", offset=LATE, align_bytes=64)
+        h_codes = [sb("h_codes0", [P, HALF], U32), sb("h_codes1", [P, HALF], U32)]
         h_scales = [sb("h_scales%d" % half, [P, HALF], U8) for half in range(2)]
         window_0 = sb("window_0", [P, T], F32, tag="w_woven")
         nc.gpsimd.memset(window_0[:].bitcast(I32), 0)
-        resid = sb("resid", [P, PACK, HALF], F32)
         probs = []
         for b in range(BLOCKS):
             half, within = b // 2, slice((b % 2) * P, (b % 2 + 1) * P)
@@ -182,10 +186,6 @@ def tile_attend_gbias_wb_log_kernel(tc, xT, wT, ts, kb, us, y, wt, offs, out_0, 
             prob = sb("prob%d" % b, [P, PACK, P], F32)
             nc.scalar.activation(prob[:], scaled[:], ACT.Sigmoid, bias=kb_col[:, b : b + 1], scale=ts_col[:, b : b + 1])
             probs.append(prob)
-        woven_factor = sb("woven_factor", [P, P, PACK], F32, tag="scaled3")
-        nc.scalar.copy(woven_factor[:], factor_ps[2][:].rearrange("m t i -> m i t"))
-        window_1 = sb("window_1", [P, T], F32, tag="w_raw0")
-        nc.gpsimd.memset(window_1[:].bitcast(I32), 0)
 
         def product(t, half, out):
             features = slice(t * P, (t + 1) * P)
@@ -199,44 +199,48 @@ def tile_attend_gbias_wb_log_kernel(tc, xT, wT, ts, kb, us, y, wt, offs, out_0, 
                 stop=True,
             )
 
-        for half in range(2):
-            blocks = (2 * half, 2 * half + 1)
-            if half:
-                h_second = sb("h_second", [P, HALF, PACK], BF16)
-                last_resid = sb("last_resid", [P, PACK, P], F32, tag="h_first0")
-                woven_resid = sb("woven_resid", [P, P, PACK], F32, tag="h_first1")
-            for b in blocks:
-                slots, within = slice(b * P, (b + 1) * P), slice((b % 2) * P, (b % 2 + 1) * P)
-                p_ps = bank("p_ps", "work")
-                for t in range(PACK):
-                    turn(p_ps[:, t, :], probs[b][:, t, :])
-                if b == 2:
-                    nc.vector.tensor_tensor(
-                        woven_resid[:].rearrange("m (c i) t -> m c t i", i=PAIR),
-                        p_ps[:].rearrange("m t (c i) -> m c t i", i=PAIR),
-                        y_raw[half][:, :, within].rearrange("m t (c i) -> m c t i", i=PAIR),
-                        ALU.subtract,
-                    )
-                else:
-                    nc.vector.tensor_tensor(last_resid[:] if half else resid[:, :, slots], p_ps[:], y_raw[half][:, :, within], ALU.subtract)
-            for b in blocks:
-                slots, within = slice(b * P, (b + 1) * P), slice((b % 2) * P, (b % 2 + 1) * P)
-                if b == 2:
-                    nc.gpsimd.tensor_tensor(h_second[:, within, :], woven_factor[:], woven_resid[:], ALU.mult)
-                    continue
-                nc.vector.tensor_tensor(
-                    (h_second[:, within, :] if half else h_first[b][:]).rearrange("m (c i) t -> m c t i", i=LINE),
-                    factor_ps[b][:].rearrange("m t (c i) -> m c t i", i=LINE),
-                    (last_resid[:] if half else resid[:, :, slots]).rearrange("m t (c i) -> m c t i", i=LINE),
-                    ALU.mult,
-                )
-            if half:
-                nc.vector.quantize_mx(h_codes[1][:].bitcast(E5), h_scales[1][:], flat(h_second))
-                continue
-            for b in blocks:
-                slots = slice(b * P, (b + 1) * P)
-                nc.vector.quantize_mx(h_codes[0][:, slots].bitcast(E5), h_scales[0][:, slots], flat(h_first[b]))
+        woven_resid = sb("woven_resid", [P, HALF, PACK], F32)
+        turned = []
+        for b in range(BLOCKS):
+            p_ps = bank("p_ps", "work")
+            for t in range(PACK):
+                turn(p_ps[:, t, :], probs[b][:, t, :])
+            turned.append(p_ps)
 
+        def y_block(b):
+            return y_raw[b // 2][:, :, (b % 2) * P : (b % 2 + 1) * P]
+
+        def weave_resid(b):
+            nc.vector.tensor_tensor(
+                woven_resid[:, b // 2 * P : (b // 2 + 1) * P, :].rearrange("m (c i) t -> m c t i", i=PAIR),
+                turned[b][:].rearrange("m t (c i) -> m c t i", i=PAIR),
+                y_block(b).rearrange("m t (c i) -> m c t i", i=PAIR),
+                ALU.subtract,
+            )
+
+        def times_factor(b, out, resid):
+            nc.vector.tensor_tensor(
+                out.rearrange("m (c i) t -> m c t i", i=LINE),
+                factor_ps[b][:].rearrange("m t (c i) -> m c t i", i=LINE),
+                resid[:].rearrange("m t (c i) -> m c t i", i=LINE),
+                ALU.mult,
+            )
+
+        weave_resid(0)
+        nc.gpsimd.tensor_tensor(h_first[:, :P, :], woven_factor[:, :P, :], woven_resid[:, :P, :], ALU.mult)
+        first_resid = sb("first_resid", [P, PACK, P], F32)
+        nc.vector.tensor_tensor(first_resid[:], turned[1][:], y_block(1), ALU.subtract)
+        weave_resid(2)
+        times_factor(1, h_first[:, P:, :], first_resid)
+        nc.vector.quantize_mx(h_codes[0][:].bitcast(E5), h_scales[0][:], flat(h_first))
+        h_second = late.tile([P, HALF, PACK], BF16, name="h_second", offset=LATE - 2 * P * PACK, align_bytes=64)
+        nc.gpsimd.tensor_tensor(h_second[:, :P, :], woven_factor[:, P:, :], woven_resid[:, P:, :], ALU.mult)
+        last_resid = late.tile([P, PACK, P], F32, name="last_resid", offset=LATE + 2 * P * PACK, align_bytes=64)
+        nc.vector.tensor_tensor(last_resid[:], turned[3][:], y_block(3), ALU.subtract)
+        times_factor(3, h_second[:, P:, :], last_resid)
+        nc.vector.quantize_mx(h_codes[1][:].bitcast(E5), h_scales[1][:], flat(h_second))
+        window_3 = late.tile([P, T], F32, name="window_3", offset=0, align_bytes=64)
+        nc.gpsimd.memset(window_3[:].bitcast(I32), 0)
         windows = [window_0, window_1, window_2, window_3]
 
         out_planes = out_0.rearrange("(p t) c -> t p c", t=PACK)
@@ -254,19 +258,17 @@ def tile_attend_gbias_wb_log_kernel(tc, xT, wT, ts, kb, us, y, wt, offs, out_0, 
             nc.vector.tensor_copy(windows[t][:].indirect(offsets[:, HALF // PER_COLUMN :]), dw[:])
             nc.sync.dma_start(out_planes[t], windows[t][:])
 
-        g_first = sb("g_first", [P, PACK, HALF], F32)
-        g_second = sb("g_second", [P, PACK, HALF], F32, tag="h_second")
-        for t in range(PACK):
-            nc.scalar.activation(g_first[:, t, :], resid[:, t, :], ACT.Copy, scale=wt_col[:, t : t + 1])
+        g = sb("g", [P, PACK, S], F32, tag="w_raw1")
         for t in range(PACK):
             scale = wt_col[:, t : t + 1]
-            nc.gpsimd.tensor_scalar(g_second[:, t, :P], woven_resid[:, :, t], scale, 0.0, ALU.mult, ALU.add)
-            nc.gpsimd.tensor_scalar(g_second[:, t, P:], last_resid[:, t, :], scale, 0.0, ALU.mult, ALU.add)
+            woven_g = g[:, t, :].rearrange("m (h b i) -> m h b i", h=2, b=2)[:, :, 0, :]
+            nc.gpsimd.tensor_scalar(woven_g, woven_resid[:, :, t].rearrange("m (h i) -> m h i", h=2), scale, 0.0, ALU.mult, ALU.add)
+            nc.gpsimd.tensor_scalar(g[:, t, P : 2 * P], first_resid[:, t, :], scale, 0.0, ALU.mult, ALU.add)
+            nc.gpsimd.tensor_scalar(g[:, t, 3 * P :], last_resid[:, t, :], scale, 0.0, ALU.mult, ALU.add)
         sum_ps = bank("sum_ps", "factor3")
         for b in range(BLOCKS):
-            g = g_second if b // 2 else g_first
             for t in range(PACK):
-                turn(sum_ps[:, b, :], g[:, t, (b % 2) * P : (b % 2 + 1) * P], start=(t == 0), stop=(t == PACK - 1))
+                turn(sum_ps[:, b, :], g[:, t, b * P : (b + 1) * P], start=(t == 0), stop=(t == PACK - 1))
         db_col = sb("db_col", [P, P], F32)
         nc.vector.memset(db_col[:], 0.0)
         copied = sb("copied", [P, P], F32, tag="dw_first3")

@@ -258,20 +258,21 @@ def tile_attend_gbias_wb_log_kernel(tc, xT, wT, ts, kb, us, y, wt, offs, out_0, 
             nc.vector.tensor_copy(windows[t][:].indirect(offsets[:, HALF // PER_COLUMN :]), dw[:])
             nc.sync.dma_start(out_planes[t], windows[t][:])
 
-        g = sb("g", [P, PACK, S], F32, tag="w_raw1")
-        for t in range(PACK):
-            scale = wt_col[:, t : t + 1]
-            woven_g = g[:, t, :].rearrange("m (h b i) -> m h b i", h=2, b=2)[:, :, 0, :]
-            nc.gpsimd.tensor_scalar(woven_g, woven_resid[:, :, t].rearrange("m (h i) -> m h i", h=2), scale, 0.0, ALU.mult, ALU.add)
-            nc.gpsimd.tensor_scalar(g[:, t, P : 2 * P], first_resid[:, t, :], scale, 0.0, ALU.mult, ALU.add)
-            nc.gpsimd.tensor_scalar(g[:, t, 3 * P :], last_resid[:, t, :], scale, 0.0, ALU.mult, ALU.add)
+        g_first = sb("g_first", [P, PACK, HALF], F32)
+        g_second = sb("g_second", [P, PACK, HALF], F32, tag="dw_first3")
+        for g, woven, planar in ((g_first, woven_resid[:, :P, :], first_resid), (g_second, woven_resid[:, P:, :], last_resid)):
+            for t in range(PACK):
+                nc.scalar.activation(g[:, t, :P], woven[:, :, t], ACT.Copy, scale=wt_col[:, t : t + 1])
+            for t in range(PACK):
+                nc.scalar.activation(g[:, t, P:], planar[:, t, :], ACT.Copy, scale=wt_col[:, t : t + 1])
         sum_ps = bank("sum_ps", "factor3")
         for b in range(BLOCKS):
+            g = g_second if b // 2 else g_first
             for t in range(PACK):
-                turn(sum_ps[:, b, :], g[:, t, b * P : (b + 1) * P], start=(t == 0), stop=(t == PACK - 1))
+                turn(sum_ps[:, b, :], g[:, t, (b % 2) * P : (b % 2 + 1) * P], start=(t == 0), stop=(t == PACK - 1))
         db_col = sb("db_col", [P, P], F32)
         nc.vector.memset(db_col[:], 0.0)
-        copied = sb("copied", [P, P], F32, tag="dw_first3")
+        copied = sb("copied", [P, P], F32, tag="dw_first2")
         for b in range(BLOCKS):
             nc.scalar.activation(copied[:], sum_ps[:, b, :], ACT.Copy, accum_out=db_col[:, b : b + 1])
         row_ps = bank("row_ps", "factor1")

@@ -26,6 +26,7 @@ PER_COLUMN = 16
 LINE = 4
 PAIR = 2
 LATE = 4 * T - 2 * P * PACK
+SHARE = 80
 LOADED = P - 1
 BANKS = {"factor0": 1, "factor1": 1, "factor2": 1, "factor3": 1, "work": 4}
 
@@ -133,9 +134,9 @@ def tile_attend_gbias_wb_log_kernel(tc, xT, wT, ts, kb, us, y, wt, offs, out_0, 
             for t in range(PACK):
                 turn(f_ps[:, t, :], factor_t[:, t, :])
             factor_ps.append(f_ps)
-        woven_factor = sb("woven_factor", [P, HALF, PACK], F32)
-        for b in range(2):
-            nc.scalar.copy(woven_factor[:, b * P : (b + 1) * P, :], factor_ps[2 * b][:].rearrange("m t i -> m i t"))
+        woven_factor = sb("woven_factor", [P, P + SHARE, PACK], F32)
+        nc.scalar.copy(woven_factor[:, :P, :], factor_ps[0][:].rearrange("m t i -> m i t"))
+        nc.scalar.copy(woven_factor[:, P:, :], factor_ps[2][:, :, :SHARE].rearrange("m t i -> m i t"))
 
         w_woven = sb("w_woven", [P, S, PACK], BF16)
         w_codes = [sb("w_codes%d" % half, [P, HALF], U32) for half in range(2)]
@@ -232,12 +233,18 @@ def tile_attend_gbias_wb_log_kernel(tc, xT, wT, ts, kb, us, y, wt, offs, out_0, 
         nc.vector.tensor_tensor(first_resid[:], turned[1][:], y_block(1), ALU.subtract)
         weave_resid(2)
         times_factor(1, h_first[:, P:, :], first_resid)
+        last_resid = sb("last_resid", [P, PACK, P], F32)
+        nc.vector.tensor_tensor(last_resid[:], turned[3][:], y_block(3), ALU.subtract)
         nc.vector.quantize_mx(h_codes[0][:].bitcast(E5), h_scales[0][:], flat(h_first))
         h_second = late.tile([P, HALF, PACK], BF16, name="h_second", offset=LATE - 2 * P * PACK, align_bytes=64)
-        nc.gpsimd.tensor_tensor(h_second[:, :P, :], woven_factor[:, P:, :], woven_resid[:, P:, :], ALU.mult)
-        last_resid = late.tile([P, PACK, P], F32, name="last_resid", offset=LATE + 2 * P * PACK, align_bytes=64)
-        nc.vector.tensor_tensor(last_resid[:], turned[3][:], y_block(3), ALU.subtract)
+        nc.gpsimd.tensor_tensor(h_second[:, :SHARE, :], woven_factor[:, P:, :], woven_resid[:, P : P + SHARE, :], ALU.mult)
         times_factor(3, h_second[:, P:, :], last_resid)
+        nc.vector.tensor_tensor(
+            h_second[:, SHARE:P, :],
+            factor_ps[2][:, :, SHARE:].rearrange("m t i -> m i t"),
+            woven_resid[:, P + SHARE :, :],
+            ALU.mult,
+        )
         nc.vector.quantize_mx(h_codes[1][:].bitcast(E5), h_scales[1][:], flat(h_second))
         window_3 = late.tile([P, T], F32, name="window_3", offset=0, align_bytes=64)
         nc.gpsimd.memset(window_3[:].bitcast(I32), 0)
@@ -259,12 +266,15 @@ def tile_attend_gbias_wb_log_kernel(tc, xT, wT, ts, kb, us, y, wt, offs, out_0, 
             nc.sync.dma_start(out_planes[t], windows[t][:])
 
         g_first = sb("g_first", [P, PACK, HALF], F32)
-        g_second = sb("g_second", [P, PACK, HALF], F32, tag="dw_first3")
-        for g, woven, planar in ((g_first, woven_resid[:, :P, :], first_resid), (g_second, woven_resid[:, P:, :], last_resid)):
-            for t in range(PACK):
-                nc.scalar.activation(g[:, t, :P], woven[:, :, t], ACT.Copy, scale=wt_col[:, t : t + 1])
-            for t in range(PACK):
-                nc.scalar.activation(g[:, t, P:], planar[:, t, :], ACT.Copy, scale=wt_col[:, t : t + 1])
+        g_second = sb("g_second", [P, PACK, HALF], F32, tag="w_raw1")
+        for t in range(PACK):
+            nc.scalar.activation(g_first[:, t, :P], woven_resid[:, :P, t], ACT.Copy, scale=wt_col[:, t : t + 1])
+        for t in range(PACK):
+            nc.scalar.activation(g_first[:, t, P:], first_resid[:, t, :], ACT.Copy, scale=wt_col[:, t : t + 1])
+        for t in range(PACK):
+            nc.gpsimd.tensor_scalar(g_second[:, t, :P], woven_resid[:, P:, t], wt_col[:, t : t + 1], 0.0, ALU.mult, ALU.add)
+        for t in range(PACK):
+            nc.gpsimd.tensor_scalar(g_second[:, t, P:], last_resid[:, t, :], wt_col[:, t : t + 1], 0.0, ALU.mult, ALU.add)
         sum_ps = bank("sum_ps", "factor3")
         for b in range(BLOCKS):
             g = g_second if b // 2 else g_first
@@ -272,7 +282,7 @@ def tile_attend_gbias_wb_log_kernel(tc, xT, wT, ts, kb, us, y, wt, offs, out_0, 
                 turn(sum_ps[:, b, :], g[:, t, (b % 2) * P : (b % 2 + 1) * P], start=(t == 0), stop=(t == PACK - 1))
         db_col = sb("db_col", [P, P], F32)
         nc.vector.memset(db_col[:], 0.0)
-        copied = sb("copied", [P, P], F32, tag="dw_first2")
+        copied = sb("copied", [P, P], F32, tag="dw_first3")
         for b in range(BLOCKS):
             nc.scalar.activation(copied[:], sum_ps[:, b, :], ACT.Copy, accum_out=db_col[:, b : b + 1])
         row_ps = bank("row_ps", "factor1")

@@ -62,8 +62,8 @@ def tile_attend_gbias_wb_log_kernel(tc, xT, wT, ts, kb, us, y, wt, offs, out_0, 
         us_col = sb("us_col", [P, PACK], F32)
         wt_col = sb("wt_col", [P, PACK], F32)
 
-        nc.sync.dma_start(x_raw[:], xT.rearrange("(p t) r -> p t r", t=PACK))
         nc.sync.dma_start(offsets[:], offs)
+        nc.sync.dma_start(x_raw[:], xT.rearrange("(p t) r -> p t r", t=PACK))
         nc.scalar.dma_start(ts_table[LOADED:P, :], ts[0:1, :])
         nc.scalar.dma_start(kb_table[LOADED:P, :], kb[0:1, :])
         nc.scalar.dma_start(us_col[:], us.rearrange("(p t) o -> p (t o)", t=PACK))
@@ -78,32 +78,27 @@ def tile_attend_gbias_wb_log_kernel(tc, xT, wT, ts, kb, us, y, wt, offs, out_0, 
         ident = sb("ident", [P, P], F32)
         make_identity(nc, ident[:])
 
-        nc.vector.memset(ts_table[0:LOADED, :].bitcast(I32), 0)
-        nc.vector.memset(kb_table[0:LOADED, :].bitcast(I32), 0)
+        nc.vector.memset(ts_table[0:LOADED, : T - 1].bitcast(I32), 0)
+        nc.vector.memset(ts_table[0:LOADED, T - 1 :].bitcast(I32), 0)
+        nc.gpsimd.memset(kb_table[0:LOADED, :].bitcast(I32), 0)
+        window_1 = sb("window_1", [P, T], F32)
+        nc.gpsimd.memset(window_1[:].bitcast(I32), 0)
+        window_2 = sb("window_2", [P, T], F32)
+        nc.gpsimd.memset(window_2[:].bitcast(I32), 0)
+        db_col = sb("db_col", [P, P], F32)
+        nc.gpsimd.memset(db_col[:], 0.0)
 
-        us_ps = bank("us_ps", "work")
-        for t in range(PACK):
-            spread(us_ps[:, t, :], us_col[:, t : t + 1])
-        us_row = sb("us_row", [P, PACK, P], F32)
-        nc.scalar.copy(us_row[:], us_ps[:])
         us_wt_col = sb("us_wt_col", [P, PACK], F32)
-        nc.vector.tensor_tensor(us_wt_col[:], us_col[:], wt_col[:], ALU.mult)
+        nc.gpsimd.tensor_tensor(us_wt_col[:], us_col[:], wt_col[:], ALU.mult)
 
-        listed_cols = []
-        for name, table in (("ts", ts_table), ("kb", kb_table)):
+        turned_cols = []
+        for name, table, tag in (("ts", ts_table, "factor0"), ("kb", kb_table, "factor1")):
             picked = sb(name + "_picked", [P, S], F32)
             nc.vector.tensor_copy(picked[:], table[:].indirect(offsets[:]))
-            col_ps = bank(name + "_ps", "work")
+            col_ps = bank(name + "_ps", tag)
             for b in range(BLOCKS):
                 turn(col_ps[:, b, :], picked[:, b * P : (b + 1) * P])
-            col = sb(name + "_col", [P, BLOCKS], F32)
-            nc.scalar.copy(col[:], col_ps[:, :, LOADED])
-            listed_cols.append(col)
-        ts_col, kb_col = listed_cols
-        window_1 = sb("window_1", [P, T], F32, tag="ts_table")
-        nc.gpsimd.memset(window_1[:].bitcast(I32), 0)
-        window_2 = sb("window_2", [P, T], F32, tag="kb_table")
-        nc.gpsimd.memset(window_2[:].bitcast(I32), 0)
+            turned_cols.append(col_ps)
 
 
         x_d = sb("x_d", [P, R, PACK], BF16)
@@ -111,6 +106,11 @@ def tile_attend_gbias_wb_log_kernel(tc, xT, wT, ts, kb, us, y, wt, offs, out_0, 
             x_d[:].rearrange("p (j m) t -> p m t j", j=PACK),
             x_raw[:].rearrange("p t (m j) -> p m t j", j=PACK),
         )
+
+        spread_out = sb("spread_out", [P, R + 2 * BLOCKS], F32, tag="x_raw")
+        ts_col, kb_col = spread_out[:, R : R + BLOCKS], spread_out[:, R + BLOCKS :]
+        nc.scalar.copy(ts_col, turned_cols[0][:, :, LOADED])
+        nc.scalar.copy(kb_col, turned_cols[1][:, :, LOADED])
 
         x_r = sb("x_r", [P, D, PACK], BF16)
         x_words = flat(x_d).bitcast(F32)
@@ -123,23 +123,30 @@ def tile_attend_gbias_wb_log_kernel(tc, xT, wT, ts, kb, us, y, wt, offs, out_0, 
                 flat(xt_ps).bitcast(BF16).rearrange("m (j p e) -> m e p j", j=PACK, e=2),
             )
 
-        us_wt_ps = bank("us_wt_ps", "work")
+        us_ps = bank("us_ps", "factor0")
+        for t in range(PACK):
+            spread(us_ps[:, t, :], us_col[:, t : t + 1])
+        us_row = spread_out[:, :R].rearrange("p (t m) -> p t m", t=PACK)
+        nc.scalar.copy(us_row, us_ps[:])
+
+        us_wt_ps = bank("us_wt_ps", "factor2")
         for t in range(PACK):
             spread(us_wt_ps[:, t, :], us_wt_col[:, t : t + 1])
+        factor_t = [sb("factor_t%d" % b, [P, PACK, P], F32) for b in range(BLOCKS)]
+        for b in range(BLOCKS):
+            nc.scalar.activation(factor_t[b][:], us_wt_ps[:], ACT.Copy, scale=ts_col[:, b : b + 1])
         factor_ps = []
         for b in range(BLOCKS):
-            factor_t = sb("factor_t%d" % b, [P, PACK, P], F32)
-            nc.scalar.activation(factor_t[:], us_wt_ps[:], ACT.Copy, scale=ts_col[:, b : b + 1])
             f_ps = bank("f_ps", "factor%d" % b)
             for t in range(PACK):
-                turn(f_ps[:, t, :], factor_t[:, t, :])
+                turn(f_ps[:, t, :], factor_t[b][:, t, :])
             factor_ps.append(f_ps)
         woven_factor = sb("woven_factor", [P, P + SHARE, PACK], F32)
         nc.scalar.copy(woven_factor[:, :P, :], factor_ps[0][:].rearrange("m t i -> m i t"))
         nc.scalar.copy(woven_factor[:, P:, :], factor_ps[2][:, :, :SHARE].rearrange("m t i -> m i t"))
 
         w_woven = sb("w_woven", [P, S, PACK], BF16)
-        w_codes = [sb("w_codes%d" % half, [P, HALF], U32) for half in range(2)]
+        w_codes = [sb("w_codes%d" % half, [P, HALF], U32, tag="factor_t%d" % (2 + half)) for half in range(2)]
         w_scales = [sb("w_scales%d" % half, [P, HALF], U8) for half in range(2)]
 
         def gather_w(t, first, last):
@@ -183,7 +190,7 @@ def tile_attend_gbias_wb_log_kernel(tc, xT, wT, ts, kb, us, y, wt, offs, out_0, 
                 stop=True,
             )
             scaled = sb("scaled%d" % b, [P, PACK, P], F32)
-            nc.vector.tensor_tensor(scaled[:], a_ps[:], us_row[:], ALU.mult)
+            nc.vector.tensor_tensor(scaled[:], a_ps[:], us_row, ALU.mult)
             prob = sb("prob%d" % b, [P, PACK, P], F32)
             nc.scalar.activation(prob[:], scaled[:], ACT.Sigmoid, bias=kb_col[:, b : b + 1], scale=ts_col[:, b : b + 1])
             probs.append(prob)
@@ -280,8 +287,6 @@ def tile_attend_gbias_wb_log_kernel(tc, xT, wT, ts, kb, us, y, wt, offs, out_0, 
             g = g_second if b // 2 else g_first
             for t in range(PACK):
                 turn(sum_ps[:, b, :], g[:, t, (b % 2) * P : (b % 2 + 1) * P], start=(t == 0), stop=(t == PACK - 1))
-        db_col = sb("db_col", [P, P], F32)
-        nc.vector.memset(db_col[:], 0.0)
         copied = sb("copied", [P, P], F32, tag="dw_first3")
         for b in range(BLOCKS):
             nc.scalar.activation(copied[:], sum_ps[:, b, :], ACT.Copy, accum_out=db_col[:, b : b + 1])

@@ -25,7 +25,8 @@ BLOCKS = S // P
 PER_COLUMN = 16
 LINE = 4
 PAIR = 2
-LATE = 4 * T - 2 * P * PACK
+WINDOW = 4 * T
+H_BYTES = 2 * HALF * PACK
 SHARE = 80
 LOADED = P - 1
 BANKS = {"factor0": 1, "factor1": 1, "factor2": 1, "factor3": 1, "work": 4}
@@ -171,7 +172,7 @@ def tile_attend_gbias_wb_log_kernel(tc, xT, wT, ts, kb, us, y, wt, offs, out_0, 
                 columns = slice((2 * half + b) * P * PACK, (2 * half + b + 1) * P * PACK)
                 nc.vector.quantize_mx(w_codes[half][:, within].bitcast(E4), w_scales[half][:, within], flat(w_woven)[:, columns])
 
-        h_first = late.tile([P, HALF, PACK], BF16, name="h_first", offset=LATE, align_bytes=64)
+        h_first = late.tile([P, HALF, PACK], BF16, name="h_first", offset=WINDOW, align_bytes=64)
         h_codes = [sb("h_codes0", [P, HALF], U32), sb("h_codes1", [P, HALF], U32)]
         h_scales = [sb("h_scales%d" % half, [P, HALF], U8) for half in range(2)]
         window_0 = sb("window_0", [P, T], F32, tag="w_woven")
@@ -243,7 +244,7 @@ def tile_attend_gbias_wb_log_kernel(tc, xT, wT, ts, kb, us, y, wt, offs, out_0, 
         last_resid = sb("last_resid", [P, PACK, P], F32)
         nc.vector.tensor_tensor(last_resid[:], turned[3][:], y_block(3), ALU.subtract)
         nc.vector.quantize_mx(h_codes[0][:].bitcast(E5), h_scales[0][:], flat(h_first))
-        h_second = late.tile([P, HALF, PACK], BF16, name="h_second", offset=LATE - 2 * P * PACK, align_bytes=64)
+        h_second = late.tile([P, HALF, PACK], BF16, name="h_second", offset=WINDOW - H_BYTES // 2, align_bytes=64)
         nc.gpsimd.tensor_tensor(h_second[:, :SHARE, :], woven_factor[:, P:, :], woven_resid[:, P : P + SHARE, :], ALU.mult)
         times_factor(3, h_second[:, P:, :], last_resid)
         nc.vector.tensor_tensor(
@@ -253,6 +254,9 @@ def tile_attend_gbias_wb_log_kernel(tc, xT, wT, ts, kb, us, y, wt, offs, out_0, 
             ALU.mult,
         )
         nc.vector.quantize_mx(h_codes[1][:].bitcast(E5), h_scales[1][:], flat(h_second))
+        g_3 = late.tile([P, PACK, P], F32, name="g_3", offset=WINDOW, align_bytes=64)
+        for t in range(PACK):
+            nc.gpsimd.tensor_scalar(g_3[:, t, :], last_resid[:, t, :], wt_col[:, t : t + 1], 0.0, ALU.mult, ALU.add)
         window_3 = late.tile([P, T], F32, name="window_3", offset=0, align_bytes=64)
         nc.gpsimd.memset(window_3[:].bitcast(I32), 0)
         windows = [window_0, window_1, window_2, window_3]
@@ -261,7 +265,10 @@ def tile_attend_gbias_wb_log_kernel(tc, xT, wT, ts, kb, us, y, wt, offs, out_0, 
         for t in range(PACK):
             o_ps = bank("o_ps", "factor%d" % t)
             product(t, 0, flat(o_ps)[:, :HALF])
-            dw = sb("dw_first%d" % t, [P, HALF], F32)
+            if t < PACK - 1:
+                dw = sb("dw_first%d" % t, [P, HALF], F32)
+            else:
+                dw = late.tile([P, HALF], F32, name="dw_last", offset=WINDOW + 2 * H_BYTES - 4 * P, align_bytes=64)
             nc.scalar.copy(dw[:], flat(o_ps)[:, :HALF])
             nc.scalar.activation(windows[t][:].indirect(offsets[:, : HALF // PER_COLUMN]), dw[:], ACT.Copy)
         for t in range(PACK):
@@ -273,22 +280,23 @@ def tile_attend_gbias_wb_log_kernel(tc, xT, wT, ts, kb, us, y, wt, offs, out_0, 
             nc.sync.dma_start(out_planes[t], windows[t][:])
 
         g_first = sb("g_first", [P, PACK, HALF], F32)
-        g_second = sb("g_second", [P, PACK, HALF], F32, tag="w_raw1")
         for t in range(PACK):
             nc.scalar.activation(g_first[:, t, :P], woven_resid[:, :P, t], ACT.Copy, scale=wt_col[:, t : t + 1])
         for t in range(PACK):
             nc.scalar.activation(g_first[:, t, P:], first_resid[:, t, :], ACT.Copy, scale=wt_col[:, t : t + 1])
+        g_2 = late.tile([P, PACK, P], F32, name="g_2", offset=WINDOW + H_BYTES, align_bytes=64)
         for t in range(PACK):
-            nc.gpsimd.tensor_scalar(g_second[:, t, :P], woven_resid[:, P:, t], wt_col[:, t : t + 1], 0.0, ALU.mult, ALU.add)
-        for t in range(PACK):
-            nc.gpsimd.tensor_scalar(g_second[:, t, P:], last_resid[:, t, :], wt_col[:, t : t + 1], 0.0, ALU.mult, ALU.add)
-        sum_ps = bank("sum_ps", "factor3")
-        for b in range(BLOCKS):
-            g = g_second if b // 2 else g_first
+            nc.scalar.activation(g_2[:, t, :], woven_resid[:, P:, t], ACT.Copy, scale=wt_col[:, t : t + 1])
+        g_blocks = [g_first[:, :, :P], g_first[:, :, P:], g_2, g_3]
+        early_ps = bank("early_ps", "factor3")
+        late_ps = bank("late_ps", "factor2")
+        copied = late.tile([P, P], F32, name="copied", offset=WINDOW + 2 * H_BYTES, align_bytes=64)
+        for b in (0, 1, 3, 2):
+            sum_ps = late_ps if b == 2 else early_ps
             for t in range(PACK):
-                turn(sum_ps[:, b, :], g[:, t, (b % 2) * P : (b % 2 + 1) * P], start=(t == 0), stop=(t == PACK - 1))
-        copied = sb("copied", [P, P], F32, tag="dw_first3")
-        for b in range(BLOCKS):
+                turn(sum_ps[:, b, :], g_blocks[b][:, t, :], start=(t == 0), stop=(t == PACK - 1))
+        for b in (0, 1, 3, 2):
+            sum_ps = late_ps if b == 2 else early_ps
             nc.scalar.activation(copied[:], sum_ps[:, b, :], ACT.Copy, accum_out=db_col[:, b : b + 1])
         row_ps = bank("row_ps", "factor1")
         turn(row_ps[:, 0, :], db_col[:])

@@ -239,6 +239,9 @@ def tile_attend_gbias_wb_log_kernel(tc, xT, wT, ts, kb, us, y, wt, offs, out_0, 
         nc.gpsimd.tensor_tensor(h_first[:, :P, :], woven_factor[:, :P, :], woven_resid[:, :P, :], ALU.mult)
         first_resid = sb("first_resid", [P, PACK, P], F32)
         nc.vector.tensor_tensor(first_resid[:], turned[1][:], y_block(1), ALU.subtract)
+        g_1 = sb("g_1", [P, PACK, P], F32)
+        for t in range(2):
+            nc.gpsimd.tensor_scalar(g_1[:, t, :], first_resid[:, t, :], wt_col[:, t : t + 1], 0.0, ALU.mult, ALU.add)
         weave_resid(2)
         times_factor(1, h_first[:, P:, :], first_resid)
         last_resid = sb("last_resid", [P, PACK, P], F32)
@@ -265,10 +268,7 @@ def tile_attend_gbias_wb_log_kernel(tc, xT, wT, ts, kb, us, y, wt, offs, out_0, 
         for t in range(PACK):
             o_ps = bank("o_ps", "factor%d" % t)
             product(t, 0, flat(o_ps)[:, :HALF])
-            if t < PACK - 1:
-                dw = sb("dw_first%d" % t, [P, HALF], F32)
-            else:
-                dw = late.tile([P, HALF], F32, name="dw_last", offset=WINDOW + 2 * H_BYTES - 4 * P, align_bytes=64)
+            dw = sb("dw_first%d" % t, [P, HALF], F32)
             nc.scalar.copy(dw[:], flat(o_ps)[:, :HALF])
             nc.scalar.activation(windows[t][:].indirect(offsets[:, : HALF // PER_COLUMN]), dw[:], ACT.Copy)
         for t in range(PACK):
@@ -279,24 +279,20 @@ def tile_attend_gbias_wb_log_kernel(tc, xT, wT, ts, kb, us, y, wt, offs, out_0, 
             nc.vector.tensor_copy(windows[t][:].indirect(offsets[:, HALF // PER_COLUMN :]), dw[:])
             nc.sync.dma_start(out_planes[t], windows[t][:])
 
-        g_first = sb("g_first", [P, PACK, HALF], F32)
-        for t in range(PACK):
-            nc.scalar.activation(g_first[:, t, :P], woven_resid[:, :P, t], ACT.Copy, scale=wt_col[:, t : t + 1])
-        for t in range(PACK):
-            nc.scalar.activation(g_first[:, t, P:], first_resid[:, t, :], ACT.Copy, scale=wt_col[:, t : t + 1])
-        g_2 = late.tile([P, PACK, P], F32, name="g_2", offset=WINDOW + H_BYTES, align_bytes=64)
-        for t in range(PACK):
-            nc.scalar.activation(g_2[:, t, :], woven_resid[:, P:, t], ACT.Copy, scale=wt_col[:, t : t + 1])
-        g_blocks = [g_first[:, :, :P], g_first[:, :, P:], g_2, g_3]
-        early_ps = bank("early_ps", "factor3")
-        late_ps = bank("late_ps", "factor2")
-        copied = late.tile([P, P], F32, name="copied", offset=WINDOW + 2 * H_BYTES, align_bytes=64)
-        for b in (0, 1, 3, 2):
-            sum_ps = late_ps if b == 2 else early_ps
+        g_woven = sb("g_woven", [P, PACK, HALF], F32)
+        for b in range(2):
+            for t in range(PACK):
+                slots = slice(b * P, (b + 1) * P)
+                nc.scalar.activation(g_woven[:, t, slots], woven_resid[:, slots, t], ACT.Copy, scale=wt_col[:, t : t + 1])
+        for t in range(2, PACK):
+            nc.scalar.activation(g_1[:, t, :], first_resid[:, t, :], ACT.Copy, scale=wt_col[:, t : t + 1])
+        g_blocks = [g_woven[:, :, :P], g_1, g_woven[:, :, P:], g_3]
+        sum_ps = bank("sum_ps", "factor3")
+        for b in range(BLOCKS):
             for t in range(PACK):
                 turn(sum_ps[:, b, :], g_blocks[b][:, t, :], start=(t == 0), stop=(t == PACK - 1))
-        for b in (0, 1, 3, 2):
-            sum_ps = late_ps if b == 2 else early_ps
+        copied = sb("copied", [P, P], F32, tag="dw_first3")
+        for b in range(BLOCKS):
             nc.scalar.activation(copied[:], sum_ps[:, b, :], ACT.Copy, accum_out=db_col[:, b : b + 1])
         row_ps = bank("row_ps", "factor1")
         turn(row_ps[:, 0, :], db_col[:])

from contextlib import ExitStack

import concourse.mybir as mybir
from concourse.masks import make_identity

D, R, S, T = 512, 512, 512, 2048
P = 128
PACK = 4
FLOPS = 2 * 2 * D * R * S
BYTES = 4 * (D * R + D * T + 2 * T + 2 * R + R * S + D * T + S) + 2 * P * (S // 16)

F32 = mybir.dt.float32
BF16 = mybir.dt.bfloat16
I32 = mybir.dt.int32
U32 = mybir.dt.uint32
U16 = mybir.dt.uint16
U8 = mybir.dt.uint8
E4 = mybir.dt.float8_e4m3fn_x4
E5 = mybir.dt.float8_e5m2_x4
ACT = mybir.ActivationFunctionType
ALU = mybir.AluOpType

HALF = S // 2
BLOCKS = S // P
PER_COLUMN = 16
LINE = 4
PAIR = 2
WINDOW = 4 * T
H_BYTES = 2 * HALF * PACK
SHARE = 80
LOADED = P - 1
BANKS = {"factor0": 1, "factor1": 1, "factor2": 1, "factor3": 1, "work": 4}


def tile_attend_gbias_wb_log_kernel(tc, xT, wT, ts, kb, us, y, wt, offs, out_0, out_1):
    nc = tc.nc
    with ExitStack() as ctx:
        keep = ctx.enter_context(tc.tile_pool(name="keep", bufs=1))
        late = ctx.enter_context(tc.tile_pool(name="late", bufs=1))
        psum = ctx.enter_context(tc.psum_pool(name="psum", bufs=4))

        def sb(name, shape, dtype, tag=None):
            return keep.tile(shape, dtype, name=name, tag=tag or name, align_bytes=64)

        def bank(name, tag):
            return psum.tile([P, PACK, P], F32, name=name, tag=tag, bufs=BANKS[tag])

        def flat(tile):
            return tile[:].rearrange("p a b -> p (a b)")

        def turn(out, in_, start=True, stop=True):
            nc.tensor.matmul(out, in_, ident[:], start=start, stop=stop, is_transpose=True)

        def spread(out, column):
            turn(out, column.to_broadcast([P, P]))

        offsets = keep.tile([P, S // PER_COLUMN], U16, name="offsets")
        x_raw = sb("x_raw", [P, PACK, R], F32)
        y_raw = [sb("y_raw%d" % half, [P, PACK, HALF], F32) for half in range(2)]
        w_raw = [sb("w_raw%d" % t, [P, T], F32) for t in range(PACK)]
        ts_table = sb("ts_table", [P, T], F32)
        kb_table = sb("kb_table", [P, T], F32)
        us_col = sb("us_col", [P, PACK], F32)
        wt_col = sb("wt_col", [P, PACK], F32)

        nc.sync.dma_start(offsets[:], offs)
        nc.sync.dma_start(x_raw[:], xT.rearrange("(p t) r -> p t r", t=PACK))
        nc.scalar.dma_start(ts_table[LOADED:P, :], ts[0:1, :])
        nc.scalar.dma_start(kb_table[LOADED:P, :], kb[0:1, :])
        nc.scalar.dma_start(us_col[:], us.rearrange("(p t) o -> p (t o)", t=PACK))
        nc.scalar.dma_start(wt_col[:], wt.rearrange("(p t) o -> p (t o)", t=PACK))
        w_planes = wT.rearrange("(p t) c -> t p c", t=PACK)
        for t in range(PACK):
            nc.sync.dma_start(w_raw[t][:], w_planes[t])
        y_planes = y.rearrange("(p t) s -> p t s", t=PACK)
        for half in range(2):
            nc.sync.dma_start(y_raw[half][:], y_planes[:, :, half * HALF : (half + 1) * HALF])

        ident = sb("ident", [P, P], F32)
        make_identity(nc, ident[:])

        nc.vector.memset(ts_table[0:LOADED, : T - 1].bitcast(I32), 0)
        nc.vector.memset(ts_table[0:LOADED, T - 1 :].bitcast(I32), 0)
        nc.gpsimd.memset(kb_table[0:LOADED, :].bitcast(I32), 0)
        window_1 = sb("window_1", [P, T], F32)
        nc.gpsimd.memset(window_1[:].bitcast(I32), 0)
        window_2 = sb("window_2", [P, T], F32)
        nc.gpsimd.memset(window_2[:].bitcast(I32), 0)
        db_col = sb("db_col", [P, P], F32)
        nc.gpsimd.memset(db_col[:], 0.0)

        us_wt_col = sb("us_wt_col", [P, PACK], F32)
        nc.gpsimd.tensor_tensor(us_wt_col[:], us_col[:], wt_col[:], ALU.mult)

        turned_cols = []
        for name, table, tag in (("ts", ts_table, "factor0"), ("kb", kb_table, "factor1")):
            picked = sb(name + "_picked", [P, S], F32)
            nc.vector.tensor_copy(picked[:], table[:].indirect(offsets[:]))
            col_ps = bank(name + "_ps", tag)
            for b in range(BLOCKS):
                turn(col_ps[:, b, :], picked[:, b * P : (b + 1) * P])
            turned_cols.append(col_ps)


        x_d = sb("x_d", [P, R, PACK], BF16)
        nc.scalar.copy(
            x_d[:].rearrange("p (j m) t -> p m t j", j=PACK),
            x_raw[:].rearrange("p t (m j) -> p m t j", j=PACK),
        )

        spread_out = sb("spread_out", [P, R + 2 * BLOCKS], F32, tag="x_raw")
        ts_col, kb_col = spread_out[:, R : R + BLOCKS], spread_out[:, R + BLOCKS :]
        nc.scalar.copy(ts_col, turned_cols[0][:, :, LOADED])
        nc.scalar.copy(kb_col, turned_cols[1][:, :, LOADED])

        x_r = sb("x_r", [P, D, PACK], BF16)
        x_words = flat(x_d).bitcast(F32)
        for u in range(2):
            xt_ps = bank("xt_ps", "factor%d" % (2 + u))
            for j in range(PACK):
                turn(xt_ps[:, j, :], x_words[:, 2 * j * P + u : 2 * (j + 1) * P : 2])
            nc.scalar.copy(
                x_r[:, 2 * u * P : 2 * (u + 1) * P, :].rearrange("m (e p) j -> m e p j", e=2),
                flat(xt_ps).bitcast(BF16).rearrange("m (j p e) -> m e p j", j=PACK, e=2),
            )

        us_ps = bank("us_ps", "factor0")
        for t in range(PACK):
            spread(us_ps[:, t, :], us_col[:, t : t + 1])
        us_row = spread_out[:, :R].rearrange("p (t m) -> p t m", t=PACK)
        nc.scalar.copy(us_row, us_ps[:])

        us_wt_ps = bank("us_wt_ps", "factor2")
        for t in range(PACK):
            spread(us_wt_ps[:, t, :], us_wt_col[:, t : t + 1])
        factor_t = [sb("factor_t%d" % b, [P, PACK, P], F32) for b in range(BLOCKS)]
        for b in range(BLOCKS):
            nc.scalar.activation(factor_t[b][:], us_wt_ps[:], ACT.Copy, scale=ts_col[:, b : b + 1])
        factor_ps = []
        for b in range(BLOCKS):
            f_ps = bank("f_ps", "factor%d" % b)
            for t in range(PACK):
                turn(f_ps[:, t, :], factor_t[b][:, t, :])
            factor_ps.append(f_ps)
        woven_factor = sb("woven_factor", [P, P + SHARE, PACK], F32)
        nc.scalar.copy(woven_factor[:, :P, :], factor_ps[0][:].rearrange("m t i -> m i t"))
        nc.scalar.copy(woven_factor[:, P:, :], factor_ps[2][:, :, :SHARE].rearrange("m t i -> m i t"))

        w_woven = sb("w_woven", [P, S, PACK], BF16)
        w_codes = [sb("w_codes%d" % half, [P, HALF], U32, tag="factor_t%d" % (2 + half)) for half in range(2)]
        w_scales = [sb("w_scales%d" % half, [P, HALF], U8) for half in range(2)]

        def gather_w(t, first, last):
            listed = offsets[:, first // PER_COLUMN : last // PER_COLUMN]
            nc.vector.tensor_copy(w_woven[:, first:last, t], w_raw[t][:].indirect(listed))

        def quantize_x(name, woven, tag):
            codes = sb(name + "_codes", [P, woven.shape[1]], U32, tag=tag)
            scales = sb(name + "_scales", [P, woven.shape[1]], U8)
            nc.vector.quantize_mx(codes[:].bitcast(E4), scales[:], flat(woven))
            return codes, scales

        gather_w(0, 0, S)
        xd_codes, xd_scales = quantize_x("xd", x_d, "w_raw0")
        gather_w(1, 0, S)
        xr_codes, xr_scales = quantize_x("xr", x_r, "w_raw1")
        gather_w(2, 0, S)
        for half in range(2):
            gather_w(PACK - 1, half * HALF, (half + 1) * HALF)
            for b in range(2):
                within = slice(b * P, (b + 1) * P)
                columns = slice((2 * half + b) * P * PACK, (2 * half + b + 1) * P * PACK)
                nc.vector.quantize_mx(w_codes[half][:, within].bitcast(E4), w_scales[half][:, within], flat(w_woven)[:, columns])

        h_first = late.tile([P, HALF, PACK], BF16, name="h_first", offset=WINDOW, align_bytes=64)
        h_codes = [sb("h_codes0", [P, HALF], U32), sb("h_codes1", [P, HALF], U32)]
        h_scales = [sb("h_scales%d" % half, [P, HALF], U8) for half in range(2)]
        window_0 = sb("window_0", [P, T], F32, tag="w_woven")
        nc.gpsimd.memset(window_0[:].bitcast(I32), 0)
        probs = []
        for b in range(BLOCKS):
            half, within = b // 2, slice((b % 2) * P, (b % 2 + 1) * P)
            a_ps = bank("a_ps", "work")
            nc.tensor.matmul_mx(
                flat(a_ps),
                lhsT=w_codes[half][:, within].bitcast(E4),
                lhsT_scale=w_scales[half][:, within],
                rhs=xd_codes[:].bitcast(E4),
                rhs_scale=xd_scales[:],
                start=True,
                stop=True,
            )
            scaled = sb("scaled%d" % b, [P, PACK, P], F32)
            nc.vector.tensor_tensor(scaled[:], a_ps[:], us_row, ALU.mult)
            prob = sb("prob%d" % b, [P, PACK, P], F32)
            nc.scalar.activation(prob[:], scaled[:], ACT.Sigmoid, bias=kb_col[:, b : b + 1], scale=ts_col[:, b : b + 1])
            probs.append(prob)

        def product(t, half, out):
            features = slice(t * P, (t + 1) * P)
            nc.tensor.matmul_mx(
                out,
                lhsT=xr_codes[:, features].bitcast(E4),
                lhsT_scale=xr_scales[:, features],
                rhs=h_codes[half][:].bitcast(E5),
                rhs_scale=h_scales[half][:],
                start=True,
                stop=True,
            )

        woven_resid = sb("woven_resid", [P, HALF, PACK], F32)
        turned = []
        for b in range(BLOCKS):
            p_ps = bank("p_ps", "work")
            for t in range(PACK):
                turn(p_ps[:, t, :], probs[b][:, t, :])
            turned.append(p_ps)

        def y_block(b):
            return y_raw[b // 2][:, :, (b % 2) * P : (b % 2 + 1) * P]

        def weave_resid(b):
            nc.vector.tensor_tensor(
                woven_resid[:, b // 2 * P : (b // 2 + 1) * P, :].rearrange("m (c i) t -> m c t i", i=PAIR),
                turned[b][:].rearrange("m t (c i) -> m c t i", i=PAIR),
                y_block(b).rearrange("m t (c i) -> m c t i", i=PAIR),
                ALU.subtract,
            )

        def times_factor(b, out, resid):
            nc.vector.tensor_tensor(
                out.rearrange("m (c i) t -> m c t i", i=LINE),
                factor_ps[b][:].rearrange("m t (c i) -> m c t i", i=LINE),
                resid[:].rearrange("m t (c i) -> m c t i", i=LINE),
                ALU.mult,
            )

        weave_resid(0)
        nc.gpsimd.tensor_tensor(h_first[:, :P, :], woven_factor[:, :P, :], woven_resid[:, :P, :], ALU.mult)
        first_resid = sb("first_resid", [P, PACK, P], F32)
        nc.vector.tensor_tensor(first_resid[:], turned[1][:], y_block(1), ALU.subtract)
        g_1 = sb("g_1", [P, PACK, P], F32)
        for t in range(2):
            nc.gpsimd.tensor_scalar(g_1[:, t, :], first_resid[:, t, :], wt_col[:, t : t + 1], 0.0, ALU.mult, ALU.add)
        weave_resid(2)
        times_factor(1, h_first[:, P:, :], first_resid)
        last_resid = sb("last_resid", [P, PACK, P], F32)
        nc.vector.tensor_tensor(last_resid[:], turned[3][:], y_block(3), ALU.subtract)
        nc.vector.quantize_mx(h_codes[0][:].bitcast(E5), h_scales[0][:], flat(h_first))
        h_second = late.tile([P, HALF, PACK], BF16, name="h_second", offset=WINDOW - H_BYTES // 2, align_bytes=64)
        nc.gpsimd.tensor_tensor(h_second[:, :SHARE, :], woven_factor[:, P:, :], woven_resid[:, P : P + SHARE, :], ALU.mult)
        times_factor(3, h_second[:, P:, :], last_resid)
        nc.vector.tensor_tensor(
            h_second[:, SHARE:P, :],
            factor_ps[2][:, :, SHARE:].rearrange("m t i -> m i t"),
            woven_resid[:, P + SHARE :, :],
            ALU.mult,
        )
        nc.vector.quantize_mx(h_codes[1][:].bitcast(E5), h_scales[1][:], flat(h_second))
        g_3 = late.tile([P, PACK, P], F32, name="g_3", offset=WINDOW, align_bytes=64)
        for t in range(PACK):
            nc.gpsimd.tensor_scalar(g_3[:, t, :], last_resid[:, t, :], wt_col[:, t : t + 1], 0.0, ALU.mult, ALU.add)
        window_3 = late.tile([P, T], F32, name="window_3", offset=0, align_bytes=64)
        nc.gpsimd.memset(window_3[:].bitcast(I32), 0)
        windows = [window_0, window_1, window_2, window_3]

        out_planes = out_0.rearrange("(p t) c -> t p c", t=PACK)
        for t in range(PACK):
            o_ps = bank("o_ps", "factor%d" % t)
            product(t, 0, flat(o_ps)[:, :HALF])
            dw = sb("dw_first%d" % t, [P, HALF], F32)
            nc.scalar.copy(dw[:], flat(o_ps)[:, :HALF])
            nc.scalar.activation(windows[t][:].indirect(offsets[:, : HALF // PER_COLUMN]), dw[:], ACT.Copy)
        for t in range(PACK):
            o_ps = bank("o_ps", "work")
            product(t, 1, flat(o_ps)[:, :HALF])
            dw = sb("dw_second%d" % t, [P, HALF], F32, tag="dw_second%d" % (t % 2))
            nc.vector.tensor_copy(dw[:], flat(o_ps)[:, :HALF])
            nc.vector.tensor_copy(windows[t][:].indirect(offsets[:, HALF // PER_COLUMN :]), dw[:])
            nc.sync.dma_start(out_planes[t], windows[t][:])

        g_woven = sb("g_woven", [P, PACK, HALF], F32)
        for b in range(2):
            for t in range(PACK):
                slots = slice(b * P, (b + 1) * P)
                nc.scalar.activation(g_woven[:, t, slots], woven_resid[:, slots, t], ACT.Copy, scale=wt_col[:, t : t + 1])
        for t in range(2, PACK):
            nc.scalar.activation(g_1[:, t, :], first_resid[:, t, :], ACT.Copy, scale=wt_col[:, t : t + 1])
        g_blocks = [g_woven[:, :, :P], g_1, g_woven[:, :, P:], g_3]
        sum_ps = bank("sum_ps", "factor3")
        for b in range(BLOCKS):
            for t in range(PACK):
                turn(sum_ps[:, b, :], g_blocks[b][:, t, :], start=(t == 0), stop=(t == PACK - 1))
        copied = sb("copied", [P, P], F32, tag="dw_first3")
        for b in range(BLOCKS):
            nc.scalar.activation(copied[:], sum_ps[:, b, :], ACT.Copy, accum_out=db_col[:, b : b + 1])
        row_ps = bank("row_ps", "factor1")
        turn(row_ps[:, 0, :], db_col[:])
        db_rows = sb("db_rows", [BLOCKS, P], F32)
        nc.scalar.copy(db_rows[:], row_ps[0:BLOCKS, 0, :])
        nc.scalar.dma_start(out_1.rearrange("o (b n) -> (o b) n", b=BLOCKS), db_rows[:])
